import numpy as np
import ml_dtypes


def mxq(x, axis, fmt="e4m3"):
    dtype, down = {"e4m3": (ml_dtypes.float8_e4m3fn, 7), "e5m2": (ml_dtypes.float8_e5m2, 14)}[fmt]
    v = np.moveaxis(np.asarray(x, np.float32).astype(ml_dtypes.bfloat16).astype(np.float64), axis, -1)
    blocks = v.reshape(v.shape[:-1] + (-1, 32))
    amax = np.abs(blocks).max(-1, keepdims=True)
    byte = np.maximum(np.where(amax > 0, np.frexp(amax)[1] - 1 + 127, 0) - down, 1)
    scale = np.exp2(byte - 127.0)
    codes = (blocks / scale).astype(np.float32).astype(dtype).astype(np.float64)
    return np.moveaxis((codes * scale).reshape(v.shape), -1, axis)


WIDE = False


def mx_kscale(k):
    if not WIDE:
        return np.ones(k)
    levels = np.array([10, -10, 5, -5, 0])
    if k % 512:
        return np.exp2(np.random.permutation(np.resize(levels, k // 32))).repeat(32)
    a = np.empty((k // 512, 16))
    for p in range(k // 512):
        a[p, :8] = np.random.permutation(np.resize(levels, 8))
        for g in range(8):
            far = levels[np.abs(levels - a[p, g]) >= 10]
            a[p, g + 8] = far[np.random.randint(len(far))]
    return np.exp2(a.ravel()).repeat(32)


def f64(x):
    return np.asarray(x).astype(np.float64)


def striped(idx):
    return np.tile(idx.reshape(-1, 16).T, (8, 1)).astype(np.uint16)


def unstriped(offs):
    return offs[:16].T.reshape(-1).astype(np.int64)


E2M1 = np.array([0.0, 0.5, 1.0, 1.5, 2.0, 3.0, 4.0, 6.0, -0.0, -0.5, -1.0, -1.5, -2.0, -3.0, -4.0, -6.0])


def pack_weight(w, fmt):
    k, n = w.shape
    w = f64(np.asarray(w, np.float32).astype(ml_dtypes.bfloat16)).reshape(k // 32, 32, n)
    amax = np.abs(w).max(1)
    if fmt == "e4m3":
        byte = np.frexp(amax)[1] - 1 + 127 - 7
    else:
        mant, ex = np.frexp(amax / 6.0)
        byte = np.where(mant > 0.5, ex, ex - 1) + 127
    byte = np.clip(np.where(amax > 0, byte, 1), 1, 254)
    scaled = (w * np.exp2(127.0 - byte)[:, None, :]).reshape(k, n).astype(np.float32)
    by_word = np.ascontiguousarray(scaled.reshape(k // 512, 128, 4, n).transpose(0, 1, 3, 2))
    if fmt == "e4m3":
        words = by_word.astype(ml_dtypes.float8_e4m3fn).view(np.uint8)
    else:
        c = by_word.astype(ml_dtypes.float4_e2m1fn).view(np.uint8) & 0xF
        words = (c[..., 0::2] | (c[..., 1::2] << 4)).reshape(k // 512, 128, 2 * n)
    return np.ascontiguousarray(words), np.ascontiguousarray(byte.astype(np.uint8).reshape(k // 512, 16, n))


def unpack_weight(words, scales, fmt):
    g, _, n = scales.shape
    words = np.ascontiguousarray(words).reshape(g, 128, n, -1)
    if fmt == "e4m3":
        vals = words.view(ml_dtypes.float8_e4m3fn).astype(np.float64)
    else:
        nib = np.empty((g, 128, n, 4), np.uint8)
        nib[..., 0::2] = words & 0xF
        nib[..., 1::2] = words >> 4
        vals = E2M1[nib]
    vals = vals * np.repeat(np.exp2(scales.astype(np.float64) - 127.0), 8, axis=1)[..., None]
    return vals.transpose(0, 1, 3, 2).reshape(g * 512, n)


def relu2(v):
    return np.maximum(v, 0.0) ** 2


def sigmoid(v):
    return 1.0 / (1.0 + np.exp(-np.maximum(v, -700.0)))


K, T, E, C, H, N = 1024, 512, 8, 128, 512, 512


def by_expert(wq, xq):
    return np.concatenate([wq[e].T @ xq[:, e * C:(e + 1) * C] for e in range(E)], axis=1)


def setup_inputs():
    n = np.random.standard_normal
    s = mx_kscale(K)
    u = mx_kscale(H)
    first = np.random.permutation(np.repeat(np.arange(E), T // E))
    second = (first + 1 + np.random.permutation(np.repeat(np.arange(E - 1), -(-T // (E - 1)))[:T])) % E
    while np.bincount(second, minlength=E).max() != T // E:
        load = np.bincount(second, minlength=E); hi, lo = int(load.argmax()), int(load.argmin())
        t = np.flatnonzero((second == hi) & (first != lo))[0]; second[t] = lo
    slot_token = np.empty(E * C, np.int64); pos = np.empty((2, T), np.int64); fill = np.zeros(E, np.int64)
    place = np.stack([np.random.permutation(C) for _ in range(E)])
    for r, deal in enumerate((first, second)):
        for t in np.random.permutation(T):
            e = deal[t]; j = e * C + place[e, fill[e]]; fill[e] += 1; slot_token[j] = t; pos[r, t] = j
    g = np.random.uniform(0.2, 0.8, T)
    x = pack_weight(n((K, T)) * s[:, None], "e4m3")
    w1 = [pack_weight(m, "e2m1") for m in n((E, K, H)) / np.sqrt(K) / s[None, :, None] * u]
    w2 = [pack_weight(m, "e2m1") for m in n((E, H, N)) / np.sqrt(H) / u[None, :, None] ** 2]
    return {
        "x_words": x[0],
        "x_scales": x[1],
        "wg": (n((K, N)) / np.sqrt(K) / s[:, None]).astype(np.float32),
        "w1_words": np.stack([m[0] for m in w1]),
        "w1_scales": np.stack([m[1] for m in w1]),
        "w2_words": np.stack([m[0] for m in w2]),
        "w2_scales": np.stack([m[1] for m in w2]),
        "gate": np.stack([np.tile(g, (128, 1)), np.tile(1.0 - g, (128, 1))]).astype(np.float32),
        "offs": striped(slot_token),
        "pos1": striped(pos[0]),
        "pos2": striped(pos[1]),
    }


def reference(x_words, x_scales, wg, w1_words, w1_scales, w2_words, w2_scales, gate, offs, pos1, pos2):
    wgq = mxq(f64(wg), 0, "e4m3")
    w1 = np.stack([unpack_weight(w1_words[e], w1_scales[e], "e2m1") for e in range(E)])
    w2 = np.stack([unpack_weight(w2_words[e], w2_scales[e], "e2m1") for e in range(E)])
    idx = unstriped(offs)
    x = unpack_weight(x_words, x_scales, "e4m3")
    o = sigmoid(wgq.T @ x)
    h = relu2(by_expert(w1, x[:, idx]))
    y = by_expert(w2, mxq(h, 0, "e4m3"))
    c = sum(f64(gate[r, :1]) * y[:, unstriped(p)] for r, p in enumerate((pos1, pos2)))
    return o * c

@@ -1,0 +1,236 @@
+from contextlib import ExitStack
+
+import concourse.mybir as mybir
+from concourse.masks import make_identity
+
+K, T, E, C, H, N = 1024, 512, 8, 128, 512, 512
+FLOPS = 2 * K * N * T + 2 * E * C * (K * H + H * N)
+
+F32 = mybir.dt.float32
+BF16 = mybir.dt.bfloat16
+I32 = mybir.dt.int32
+U32 = mybir.dt.uint32
+U16 = mybir.dt.uint16
+U8 = mybir.dt.uint8
+FP8X4 = mybir.dt.float8_e4m3fn_x4
+FP4X4 = mybir.dt.float4_e2m1fn_x4
+ACT = mybir.ActivationFunctionType
+ALU = mybir.AluOpType
+
+P = 128
+PACK = 4
+PASSES = K // (P * PACK)
+PAIR = 2
+SLOTS = E * C
+BLOCKS = N // P
+HALF = N // 2
+GATHER_GROUPS = ((0, 2), (2, 4), (4, 6), (6, 7), (7, 8))
+QUANT_GROUPS = ((0, 4), (4, 6), (6, 7), (7, 8))
+
+
+def load_scale_rows(nc, plane, rows):
+    for r in range(4):
+        nc.sync.dma_start(out=plane[r:P:32, :, :].bitcast(I32), in_=rows[r].bitcast(I32))
+
+
+def tile_moe_ogt_relu2_sigmoid_kernel(
+    tc, x_words, x_scales, wg, w1_words, w1_scales, w2_words, w2_scales, gate, offs, pos1, pos2, out
+):
+    nc = tc.nc
+    with ExitStack() as ctx:
+        keep = ctx.enter_context(tc.tile_pool(name="keep", bufs=1))
+        ring = ctx.enter_context(tc.tile_pool(name="ring", bufs=2))
+        psum = ctx.enter_context(tc.psum_pool(name="psum", bufs=1))
+        banks = [psum.tile([P, 512], F32, name="bank%d" % b) for b in range(8)]
+
+        x_plane = keep.tile([P, PASSES, T], U8, name="x_plane", align_bytes=64)
+        w1_plane = keep.tile([P, E * PASSES, H], U8, name="w1_plane", align_bytes=64)
+        w2_plane = keep.tile([P, E, N], U8, name="w2_plane", align_bytes=64)
+        nc.vector.memset(x_plane[:].rearrange("p s t -> p (s t)").bitcast(I32), 0)
+        nc.vector.memset(w1_plane[:].rearrange("p s t -> p (s t)").bitcast(I32), 0)
+        nc.vector.memset(w2_plane[:].rearrange("p s t -> p (s t)").bitcast(I32), 0)
+
+        warm_in = keep.tile([P, 1], F32, name="warm_in")
+        warm_out = keep.tile([P, 1], F32, name="warm_out")
+        nc.gpsimd.memset(warm_in[:], 0.0)
+        nc.scalar.activation(out=warm_out[:], in_=warm_in[:], func=ACT.Sigmoid)
+
+        ident = keep.tile([P, P], F32, name="ident")
+        make_identity(nc, ident[:])
+
+        slot_list = keep.tile([P, SLOTS // 16], U16, name="slot_list")
+        nc.sync.dma_start(slot_list[:], offs)
+        xw = [keep.tile([P, T], I32, name="xw%d" % s, align_bytes=64) for s in range(PASSES)]
+        nc.sync.dma_start(out=xw[0][:], in_=x_words[0].rearrange("p t d -> p (t d)").bitcast(I32))
+        load_scale_rows(nc, x_plane, x_scales.rearrange("s (q r) t -> r q s t", r=4))
+        nc.sync.dma_start(out=xw[1][:], in_=x_words[1].rearrange("p t d -> p (t d)").bitcast(I32))
+
+        w1 = [keep.tile([P, PAIR * PASSES, 2 * H], U8, name="w1_%d" % q, align_bytes=64) for q in range(E // PAIR)]
+
+        def load_w1(q):
+            src = w1_words[PAIR * q : PAIR * (q + 1)].rearrange("e s p b -> p (e s) b")
+            nc.sync.dma_start(out=w1[q][:].bitcast(I32), in_=src.bitcast(I32))
+
+        load_w1(0)
+        load_scale_rows(nc, w1_plane, w1_scales.rearrange("e s (q r) i -> r q (e s) i", r=4))
+        for q in range(1, E // PAIR):
+            load_w1(q)
+        load_scale_rows(nc, w2_plane, w2_scales.rearrange("e s (q r) i -> r q (e s) i", r=4))
+        w2 = keep.tile([P, E, 2 * N], U8, name="w2", align_bytes=64)
+        nc.sync.dma_start(out=w2[:].bitcast(I32), in_=w2_words.rearrange("e s p b -> p (e s) b").bitcast(I32))
+        back = [keep.tile([P, T // 16], U16, name="back%d" % r) for r in range(2)]
+        nc.sync.dma_start(back[0][:], pos1)
+        nc.sync.dma_start(back[1][:], pos2)
+        gates = [keep.tile([P, T], F32, name="gate%d" % r) for r in range(2)]
+        for r in range(2):
+            nc.sync.dma_start(out=gates[r][:], in_=gate[r])
+        wg_raw = {}
+        for h in range(2):
+            for s in range(PASSES):
+                wg_raw[h, s] = keep.tile([P, PACK, HALF], F32, name="wg_raw%d%d" % (h, s))
+                src = wg[s * 512 : (s + 1) * 512, h * HALF : (h + 1) * HALF].rearrange("(p j) n -> p j n", j=PACK)
+                nc.sync.dma_start(out=wg_raw[h, s][:], in_=src)
+
+        tokens = {}
+        for first, last in GATHER_GROUPS:
+            width = (last - first) * C
+            picks = slot_list[:, first * C // 16 : last * C // 16]
+            for s in range(PASSES):
+                gw = keep.tile([P, width], U32, name="gw%d%d" % (first, s), align_bytes=64)
+                gs = keep.tile([P, width], U8, name="gs%d%d" % (first, s), align_bytes=64)
+                nc.vector.tensor_copy(out=gw[:], in_=xw[s][:].bitcast(U32).indirect(picks))
+                nc.vector.tensor_copy(out=gs[:], in_=x_plane[:, s, :].indirect(picks))
+                for e in range(first, last):
+                    cols = slice((e - first) * C, (e - first + 1) * C)
+                    tokens[e, s] = (gw[:, cols], gs[:, cols])
+
+        hidden, quantised = {}, {}
+        for first, last in QUANT_GROUPS:
+            tile = keep.tile([P, last - first, C * PACK], BF16, name="hidden%d" % first, align_bytes=64)
+            for e in range(first, last):
+                hidden[e] = tile
+
+        def quantise_hidden(first, last):
+            width = (last - first) * C
+            codes = keep.tile([P, width], U32, name="h_codes%d" % first, align_bytes=64)
+            plane = keep.tile([P, width], U8, name="h_plane%d" % first, align_bytes=64)
+            nc.vector.quantize_mx(
+                out=codes[:].bitcast(FP8X4), scales=plane[:], in_=hidden[first][:].rearrange("p e c -> p (e c)")
+            )
+            for e in range(first, last):
+                cols = slice((e - first) * C, (e - first + 1) * C)
+                quantised[e] = (codes[:, cols], plane[:, cols])
+
+        def first_layer(e):
+            pre = banks[e % 2]
+            for s in range(PASSES):
+                nc.tensor.matmul_mx(
+                    out=pre[:],
+                    lhsT=tokens[e, s][0].bitcast(FP8X4),
+                    lhsT_scale=tokens[e, s][1],
+                    rhs=w1[e // PAIR][:, (e % PAIR) * PASSES + s, :].bitcast(FP4X4),
+                    rhs_scale=w1_plane[:, e * PASSES + s, :],
+                    start=(s == 0),
+                    stop=(s == PASSES - 1),
+                )
+            rect = ring.tile([P, PACK, P], F32, name="rect")
+            src = pre[:].rearrange("c (p t) -> c t p", t=PACK)
+            if e == E - 1:
+                nc.vector.tensor_scalar_max(out=rect[:], in0=src, scalar1=0.0)
+            else:
+                nc.scalar.activation(out=rect[:], in_=src, func=ACT.Relu)
+            turned = banks[2 + e % 2]
+            for t in range(PACK):
+                nc.tensor.transpose(turned[:, t * C : (t + 1) * C], rect[:, t, :], ident[:])
+            first = [g[0] for g in QUANT_GROUPS if g[0] <= e][-1]
+            nc.scalar.activation(
+                out=hidden[e][:, e - first, :].rearrange("p (c t) -> p c t", t=PACK),
+                in_=turned[:].rearrange("p (t c) -> p c t", t=PACK),
+                func=ACT.Square,
+            )
+
+        for first, last in QUANT_GROUPS:
+            for e in range(first, last):
+                first_layer(e)
+            quantise_hidden(first, last)
+
+        ys = [keep.tile([P, SLOTS], F32, name="y%d" % j) for j in range(BLOCKS)]
+
+        def second_layer(j, first, last, bank, on_vector):
+            for e in range(first, last):
+                nc.tensor.matmul_mx(
+                    out=bank[:, (e - first) * C : (e - first + 1) * C],
+                    lhsT=w2[:, e, 2 * j * P : 2 * (j + 1) * P].bitcast(FP4X4),
+                    lhsT_scale=w2_plane[:, e, j * P : (j + 1) * P],
+                    rhs=quantised[e][0].bitcast(FP8X4),
+                    rhs_scale=quantised[e][1],
+                    start=True,
+                    stop=True,
+                )
+            dst, src = ys[j][:, first * C : last * C], bank[:, : (last - first) * C]
+            if on_vector:
+                nc.vector.tensor_copy(out=dst, in_=src)
+            else:
+                nc.scalar.copy(out=dst, in_=src)
+
+        second_layer(0, 0, 4, banks[0], True)
+        second_layer(0, 4, 7, banks[1], True)
+        second_layer(0, 7, 8, banks[2], False)
+        for n, (j, first) in enumerate((j, first) for j in range(1, BLOCKS) for first in (0, 4)):
+            second_layer(j, first, first + 4, banks[(3 + n) % 4], False)
+
+        opened = [keep.tile([P, T], F32, name="o%d" % j) for j in range(BLOCKS)]
+
+        def output_gate(h):
+            codes, planes = [], []
+            for s in range(PASSES):
+                woven = keep.tile([P, HALF, PACK], BF16, name="woven%d%d" % (h, s), tag="woven%d%d" % (h, s), align_bytes=64)
+                nc.scalar.copy(
+                    out=woven[:].rearrange("p (c i) j -> p c j i", i=4),
+                    in_=wg_raw[h, s][:].rearrange("p j (c i) -> p c j i", i=4),
+                )
+                gc = keep.tile([P, HALF], U32, name="wg_codes%d%d" % (h, s), align_bytes=64)
+                gp = keep.tile([P, HALF], U8, name="wg_plane%d%d" % (h, s), align_bytes=64)
+                nc.vector.quantize_mx(out=gc[:].bitcast(FP8X4), scales=gp[:], in_=woven[:].rearrange("p c j -> p (c j)"))
+                codes.append(gc)
+                planes.append(gp)
+            for u in range(2):
+                j = 2 * h + u
+                for s in range(PASSES):
+                    nc.tensor.matmul_mx(
+                        out=banks[4 + j][:],
+                        lhsT=codes[s][:, u * P : (u + 1) * P].bitcast(FP8X4),
+                        lhsT_scale=planes[s][:, u * P : (u + 1) * P],
+                        rhs=xw[s][:].bitcast(FP8X4),
+                        rhs_scale=x_plane[:, s, :],
+                        start=(s == 0),
+                        stop=(s == PASSES - 1),
+                    )
+                nc.scalar.activation(out=opened[j][:], in_=banks[4 + j][:], func=ACT.Sigmoid)
+
+        sums = {}
+
+        def combine(j, tags):
+            parts = []
+            for r in range(2):
+                part = keep.tile([P, T], F32, name="part%d%d" % (j, r), tag=tags[r], align_bytes=64)
+                nc.vector.tensor_tensor(part[:], ys[j][:].indirect(back[r][:]), gates[r][:], ALU.mult)
+                parts.append(part)
+            sums[j] = keep.tile([P, T], F32, name="sum%d" % j, tag="sum%d" % j, align_bytes=64)
+            nc.vector.tensor_tensor(sums[j][:], parts[0][:], parts[1][:], ALU.add)
+
+        def finish(j):
+            res = keep.tile([P, T], F32, name="res%d" % j)
+            nc.vector.tensor_tensor(res[:], sums[j][:], opened[j][:], ALU.mult)
+            nc.sync.dma_start(out=out[j * P : (j + 1) * P, :], in_=res[:])
+
+        combine(0, ("p00", "p01"))
+        combine(1, ("p10", "p11"))
+        output_gate(0)
+        combine(2, ("woven01", "p21"))
+        finish(0)
+        finish(1)
+        output_gate(1)
+        combine(3, ("woven11", "sum1"))
+        finish(2)
+        finish(3)

@@ -25,12 +25,14 @@ SLOTS = E * C
 BLOCKS = N // P
 HALF = N // 2
 GATHER_GROUPS = ((0, 2), (2, 4), (4, 6), (6, 7), (7, 8))
+W1_SCALE_GROUPS = ((0, 4), (4, 8))
+AHEAD = 2
 QUANT_GROUPS = ((0, 4), (4, 6), (6, 7), (7, 8))
 
 
-def load_scale_rows(nc, plane, rows):
+def load_scale_rows(queue, plane, rows):
     for r in range(4):
-        nc.sync.dma_start(out=plane[r:P:32, :, :].bitcast(I32), in_=rows[r].bitcast(I32))
+        queue.dma_start(out=plane[r:P:32, :, :].bitcast(I32), in_=rows[r].bitcast(I32))
 
 
 def tile_moe_ogt_relu2_sigmoid_kernel(
@@ -39,15 +41,19 @@ def tile_moe_ogt_relu2_sigmoid_kernel(
     nc = tc.nc
     with ExitStack() as ctx:
         keep = ctx.enter_context(tc.tile_pool(name="keep", bufs=1))
-        ring = ctx.enter_context(tc.tile_pool(name="ring", bufs=2))
+        ring = ctx.enter_context(tc.tile_pool(name="ring", bufs=3))
         psum = ctx.enter_context(tc.psum_pool(name="psum", bufs=1))
         banks = [psum.tile([P, 512], F32, name="bank%d" % b) for b in range(8)]
 
         x_plane = keep.tile([P, PASSES, T], U8, name="x_plane", align_bytes=64)
-        w1_plane = keep.tile([P, E * PASSES, H], U8, name="w1_plane", align_bytes=64)
+        w1_planes = [
+            keep.tile([P, (last - first) * PASSES, H], U8, name="w1_plane%d" % first, align_bytes=64)
+            for first, last in W1_SCALE_GROUPS
+        ]
         w2_plane = keep.tile([P, E, N], U8, name="w2_plane", align_bytes=64)
-        nc.vector.memset(x_plane[:].rearrange("p s t -> p (s t)").bitcast(I32), 0)
-        nc.vector.memset(w1_plane[:].rearrange("p s t -> p (s t)").bitcast(I32), 0)
+        nc.gpsimd.memset(x_plane[:].rearrange("p s t -> p (s t)").bitcast(I32), 0)
+        for plane in w1_planes:
+            nc.vector.memset(plane[:].rearrange("p s t -> p (s t)").bitcast(I32), 0)
         nc.vector.memset(w2_plane[:].rearrange("p s t -> p (s t)").bitcast(I32), 0)
 
         warm_in = keep.tile([P, 1], F32, name="warm_in")
@@ -59,11 +65,12 @@ def tile_moe_ogt_relu2_sigmoid_kernel(
         make_identity(nc, ident[:])
 
         slot_list = keep.tile([P, SLOTS // 16], U16, name="slot_list")
+        back = [keep.tile([P, T // 16], U16, name="back%d" % r) for r in range(2)]
+        nc.sync.dma_start(back[0][:], pos1)
+        xw = keep.tile([P, PASSES, T], I32, name="xw", align_bytes=64)
+        nc.sync.dma_start(out=xw[:], in_=x_words.rearrange("s p t d -> p s (t d)").bitcast(I32))
+        load_scale_rows(nc.sync, x_plane, x_scales.rearrange("s (q r) t -> r q s t", r=4))
         nc.sync.dma_start(slot_list[:], offs)
-        xw = [keep.tile([P, T], I32, name="xw%d" % s, align_bytes=64) for s in range(PASSES)]
-        nc.sync.dma_start(out=xw[0][:], in_=x_words[0].rearrange("p t d -> p (t d)").bitcast(I32))
-        load_scale_rows(nc, x_plane, x_scales.rearrange("s (q r) t -> r q s t", r=4))
-        nc.sync.dma_start(out=xw[1][:], in_=x_words[1].rearrange("p t d -> p (t d)").bitcast(I32))
 
         w1 = [keep.tile([P, PAIR * PASSES, 2 * H], U8, name="w1_%d" % q, align_bytes=64) for q in range(E // PAIR)]
 
@@ -71,23 +78,27 @@ def tile_moe_ogt_relu2_sigmoid_kernel(
             src = w1_words[PAIR * q : PAIR * (q + 1)].rearrange("e s p b -> p (e s) b")
             nc.sync.dma_start(out=w1[q][:].bitcast(I32), in_=src.bitcast(I32))
 
-        load_w1(0)
-        load_scale_rows(nc, w1_plane, w1_scales.rearrange("e s (q r) i -> r q (e s) i", r=4))
-        for q in range(1, E // PAIR):
-            load_w1(q)
-        load_scale_rows(nc, w2_plane, w2_scales.rearrange("e s (q r) i -> r q (e s) i", r=4))
-        w2 = keep.tile([P, E, 2 * N], U8, name="w2", align_bytes=64)
-        nc.sync.dma_start(out=w2[:].bitcast(I32), in_=w2_words.rearrange("e s p b -> p (e s) b").bitcast(I32))
-        back = [keep.tile([P, T // 16], U16, name="back%d" % r) for r in range(2)]
-        nc.sync.dma_start(back[0][:], pos1)
+        w1_scale = {}
+        for n, (first, last) in enumerate(W1_SCALE_GROUPS):
+            load_w1(2 * n)
+            load_scale_rows(nc.sync, w1_planes[n], w1_scales[first:last].rearrange("e s (q r) i -> r q (e s) i", r=4))
+            load_w1(2 * n + 1)
+            for e in range(first, last):
+                for s in range(PASSES):
+                    w1_scale[e, s] = w1_planes[n][:, (e - first) * PASSES + s, :]
+        load_scale_rows(nc.sync, w2_plane, w2_scales.rearrange("e s (q r) i -> r q (e s) i", r=4))
+        w2 = [keep.tile([P, 4, 2 * N], U8, name="w2_%d" % q, align_bytes=64) for q in range(E // 4)]
+        for q in range(E // 4):
+            src = w2_words[4 * q : 4 * (q + 1)].rearrange("e s p b -> p (e s) b")
+            nc.sync.dma_start(out=w2[q][:].bitcast(I32), in_=src.bitcast(I32))
         nc.sync.dma_start(back[1][:], pos2)
-        gates = [keep.tile([P, T], F32, name="gate%d" % r) for r in range(2)]
-        for r in range(2):
-            nc.sync.dma_start(out=gates[r][:], in_=gate[r])
+        gates = keep.tile([P, 2, T], F32, name="gates")
+        nc.sync.dma_start(out=gates[:], in_=gate.rearrange("r p t -> p r t"))
         wg_raw = {}
         for h in range(2):
             for s in range(PASSES):
-                wg_raw[h, s] = keep.tile([P, PACK, HALF], F32, name="wg_raw%d%d" % (h, s))
+                tag = {(0, 1): "stage1", (1, 1): "stage2"}.get((h, s), "wg_raw%d%d" % (h, s))
+                wg_raw[h, s] = keep.tile([P, PACK, HALF], F32, name="wg_raw%d%d" % (h, s), tag=tag, align_bytes=64)
                 src = wg[s * 512 : (s + 1) * 512, h * HALF : (h + 1) * HALF].rearrange("(p j) n -> p j n", j=PACK)
                 nc.sync.dma_start(out=wg_raw[h, s][:], in_=src)
 
@@ -98,7 +109,7 @@ def tile_moe_ogt_relu2_sigmoid_kernel(
             for s in range(PASSES):
                 gw = keep.tile([P, width], U32, name="gw%d%d" % (first, s), align_bytes=64)
                 gs = keep.tile([P, width], U8, name="gs%d%d" % (first, s), align_bytes=64)
-                nc.vector.tensor_copy(out=gw[:], in_=xw[s][:].bitcast(U32).indirect(picks))
+                nc.vector.tensor_copy(out=gw[:], in_=xw[:, s, :].bitcast(U32).indirect(picks))
                 nc.vector.tensor_copy(out=gs[:], in_=x_plane[:, s, :].indirect(picks))
                 for e in range(first, last):
                     cols = slice((e - first) * C, (e - first + 1) * C)
@@ -106,7 +117,8 @@ def tile_moe_ogt_relu2_sigmoid_kernel(
 
         hidden, quantised = {}, {}
         for first, last in QUANT_GROUPS:
-            tile = keep.tile([P, last - first, C * PACK], BF16, name="hidden%d" % first, align_bytes=64)
+            tag = "stage0" if last == E else "hidden%d" % first
+            tile = keep.tile([P, last - first, C * PACK], BF16, name="hidden%d" % first, tag=tag, align_bytes=64)
             for e in range(first, last):
                 hidden[e] = tile
 
@@ -121,15 +133,17 @@ def tile_moe_ogt_relu2_sigmoid_kernel(
                 cols = slice((e - first) * C, (e - first + 1) * C)
                 quantised[e] = (codes[:, cols], plane[:, cols])
 
-        def first_layer(e):
-            pre = banks[e % 2]
+        rects = {}
+
+        def rectify(e):
+            pre = banks[e % 3]
             for s in range(PASSES):
                 nc.tensor.matmul_mx(
                     out=pre[:],
                     lhsT=tokens[e, s][0].bitcast(FP8X4),
                     lhsT_scale=tokens[e, s][1],
                     rhs=w1[e // PAIR][:, (e % PAIR) * PASSES + s, :].bitcast(FP4X4),
-                    rhs_scale=w1_plane[:, e * PASSES + s, :],
+                    rhs_scale=w1_scale[e, s],
                     start=(s == 0),
                     stop=(s == PASSES - 1),
                 )
@@ -139,7 +153,11 @@ def tile_moe_ogt_relu2_sigmoid_kernel(
                 nc.vector.tensor_scalar_max(out=rect[:], in0=src, scalar1=0.0)
             else:
                 nc.scalar.activation(out=rect[:], in_=src, func=ACT.Relu)
-            turned = banks[2 + e % 2]
+            rects[e] = rect
+
+        def square(e):
+            rect = rects[e]
+            turned = banks[3 + e % 3]
             for t in range(PACK):
                 nc.tensor.transpose(turned[:, t * C : (t + 1) * C], rect[:, t, :], ident[:])
             first = [g[0] for g in QUANT_GROUPS if g[0] <= e][-1]
@@ -149,10 +167,14 @@ def tile_moe_ogt_relu2_sigmoid_kernel(
                 func=ACT.Square,
             )
 
-        for first, last in QUANT_GROUPS:
-            for e in range(first, last):
-                first_layer(e)
-            quantise_hidden(first, last)
+        for step in range(E + AHEAD):
+            if step < E:
+                rectify(step)
+            if step >= AHEAD:
+                square(step - AHEAD)
+                for first, last in QUANT_GROUPS:
+                    if last - 1 == step - AHEAD:
+                        quantise_hidden(first, last)
 
         ys = [keep.tile([P, SLOTS], F32, name="y%d" % j) for j in range(BLOCKS)]
 
@@ -160,7 +182,7 @@ def tile_moe_ogt_relu2_sigmoid_kernel(
             for e in range(first, last):
                 nc.tensor.matmul_mx(
                     out=bank[:, (e - first) * C : (e - first + 1) * C],
-                    lhsT=w2[:, e, 2 * j * P : 2 * (j + 1) * P].bitcast(FP4X4),
+                    lhsT=w2[e // 4][:, e % 4, 2 * j * P : 2 * (j + 1) * P].bitcast(FP4X4),
                     lhsT_scale=w2_plane[:, e, j * P : (j + 1) * P],
                     rhs=quantised[e][0].bitcast(FP8X4),
                     rhs_scale=quantised[e][1],
@@ -173,64 +195,93 @@ def tile_moe_ogt_relu2_sigmoid_kernel(
             else:
                 nc.scalar.copy(out=dst, in_=src)
 
-        second_layer(0, 0, 4, banks[0], True)
-        second_layer(0, 4, 7, banks[1], True)
-        second_layer(0, 7, 8, banks[2], False)
-        for n, (j, first) in enumerate((j, first) for j in range(1, BLOCKS) for first in (0, 4)):
-            second_layer(j, first, first + 4, banks[(3 + n) % 4], False)
+        second_layer(0, 0, 4, banks[1], True)
+        second_layer(0, 4, 7, banks[3], False)
+        second_layer(0, 7, 8, banks[0], False)
+        second_layer(1, 0, 4, banks[4], False)
+        second_layer(1, 4, 8, banks[1], False)
+        second_layer(2, 0, 4, banks[3], False)
+        second_layer(2, 4, 8, banks[0], False)
 
         opened = [keep.tile([P, T], F32, name="o%d" % j) for j in range(BLOCKS)]
 
-        def output_gate(h):
-            codes, planes = [], []
+        def quantise_gate_matrix(h):
+            woven = keep.tile([P, PASSES, HALF * PACK], BF16, name="woven%d" % h, tag="stage%d" % h, align_bytes=64)
             for s in range(PASSES):
-                woven = keep.tile([P, HALF, PACK], BF16, name="woven%d%d" % (h, s), tag="woven%d%d" % (h, s), align_bytes=64)
                 nc.scalar.copy(
-                    out=woven[:].rearrange("p (c i) j -> p c j i", i=4),
+                    out=woven[:, s, :].rearrange("p (c i j) -> p c j i", i=4, j=PACK),
                     in_=wg_raw[h, s][:].rearrange("p j (c i) -> p c j i", i=4),
                 )
-                gc = keep.tile([P, HALF], U32, name="wg_codes%d%d" % (h, s), align_bytes=64)
-                gp = keep.tile([P, HALF], U8, name="wg_plane%d%d" % (h, s), align_bytes=64)
-                nc.vector.quantize_mx(out=gc[:].bitcast(FP8X4), scales=gp[:], in_=woven[:].rearrange("p c j -> p (c j)"))
-                codes.append(gc)
-                planes.append(gp)
-            for u in range(2):
-                j = 2 * h + u
-                for s in range(PASSES):
-                    nc.tensor.matmul_mx(
-                        out=banks[4 + j][:],
-                        lhsT=codes[s][:, u * P : (u + 1) * P].bitcast(FP8X4),
-                        lhsT_scale=planes[s][:, u * P : (u + 1) * P],
-                        rhs=xw[s][:].bitcast(FP8X4),
-                        rhs_scale=x_plane[:, s, :],
-                        start=(s == 0),
-                        stop=(s == PASSES - 1),
-                    )
-                nc.scalar.activation(out=opened[j][:], in_=banks[4 + j][:], func=ACT.Sigmoid)
+            codes = keep.tile([P, PASSES, HALF], U32, name="wg_codes%d" % h, align_bytes=64)
+            planes = keep.tile([P, PASSES, HALF], U8, name="wg_plane%d" % h, align_bytes=64)
+            nc.vector.quantize_mx(
+                out=codes[:].rearrange("p s c -> p (s c)").bitcast(FP8X4),
+                scales=planes[:].rearrange("p s c -> p (s c)"),
+                in_=woven[:].rearrange("p s c -> p (s c)"),
+            )
+            return codes, planes
 
-        sums = {}
+        def output_gate(j, matrix, bank):
+            codes, planes = matrix
+            cols = slice((j % 2) * P, (j % 2 + 1) * P)
+            for s in range(PASSES):
+                nc.tensor.matmul_mx(
+                    out=bank[:],
+                    lhsT=codes[:, s, cols].bitcast(FP8X4),
+                    lhsT_scale=planes[:, s, cols],
+                    rhs=xw[:, s, :].bitcast(FP8X4),
+                    rhs_scale=x_plane[:, s, :],
+                    start=(s == 0),
+                    stop=(s == PASSES - 1),
+                )
+            nc.scalar.activation(out=opened[j][:], in_=bank[:], func=ACT.Sigmoid)
 
-        def combine(j, tags):
+        def fetch(j, first_tag):
             parts = []
             for r in range(2):
-                part = keep.tile([P, T], F32, name="part%d%d" % (j, r), tag=tags[r], align_bytes=64)
-                nc.vector.tensor_tensor(part[:], ys[j][:].indirect(back[r][:]), gates[r][:], ALU.mult)
+                tag = first_tag if r == 0 else "second%d" % j
+                part = keep.tile([P, T], F32, name="part%d%d" % (j, r), tag=tag, align_bytes=64)
+                nc.vector.tensor_tensor(part[:], ys[j][:].indirect(back[r][:]), gates[:, r, :], ALU.mult)
                 parts.append(part)
-            sums[j] = keep.tile([P, T], F32, name="sum%d" % j, tag="sum%d" % j, align_bytes=64)
-            nc.vector.tensor_tensor(sums[j][:], parts[0][:], parts[1][:], ALU.add)
+            return parts
 
-        def finish(j):
+        def add_on_vector(j, parts):
+            total = keep.tile([P, T], F32, name="sum%d" % j)
+            nc.vector.tensor_tensor(total[:], parts[0][:], parts[1][:], ALU.add)
+            return total
+
+        def add_turned(parts, bank):
+            for c in range(T // P):
+                cols = slice(c * P, (c + 1) * P)
+                for r in range(2):
+                    nc.tensor.matmul(bank[:, cols], parts[r][:, cols], ident[:], start=(r == 0), stop=(r == 1), is_transpose=True)
+
+        def turn_back(staged, bank):
+            nc.scalar.copy(out=staged, in_=bank[:])
+            for c in range(T // P):
+                cols = slice(c * P, (c + 1) * P)
+                nc.tensor.transpose(bank[:, cols], staged[:, cols], ident[:])
+            return bank
+
+        def finish(j, total):
             res = keep.tile([P, T], F32, name="res%d" % j)
-            nc.vector.tensor_tensor(res[:], sums[j][:], opened[j][:], ALU.mult)
+            nc.vector.tensor_tensor(res[:], total[:], opened[j][:], ALU.mult)
             nc.sync.dma_start(out=out[j * P : (j + 1) * P, :], in_=res[:])
 
-        combine(0, ("p00", "p01"))
-        combine(1, ("p10", "p11"))
-        output_gate(0)
-        combine(2, ("woven01", "p21"))
-        finish(0)
-        finish(1)
-        output_gate(1)
-        combine(3, ("woven11", "sum1"))
-        finish(2)
-        finish(3)
+        totals = {}
+        for j in range(2):
+            add_turned(fetch(j, "first%d" % j), banks[6 + j])
+        low = quantise_gate_matrix(0)
+        parts = fetch(2, "stage0")
+        high = quantise_gate_matrix(1)
+        totals[2] = add_on_vector(2, parts)
+        second_layer(3, 0, 4, banks[4], False)
+        second_layer(3, 4, 8, banks[1], False)
+        totals[3] = add_on_vector(3, fetch(3, "stage1"))
+        staged = keep.tile([P, 2, T], F32, name="staged", tag="stage2", align_bytes=64)
+        for j in range(2):
+            totals[j] = turn_back(staged[:, j, :], banks[6 + j])
+        for j, bank in enumerate((2, 5, 3, 0)):
+            output_gate(j, (low, high)[j // 2], banks[bank])
+        for j in range(BLOCKS):
+            finish(j, totals[j])

@@ -20,13 +20,12 @@ ALU = mybir.AluOpType
 P = 128
 PACK = 4
 PASSES = K // (P * PACK)
-PAIR = 2
 SLOTS = E * C
 BLOCKS = N // P
 HALF = N // 2
-GATHER_GROUPS = ((0, 2), (2, 4), (4, 6), (6, 7), (7, 8))
-W1_SCALE_GROUPS = ((0, 4), (4, 8))
-AHEAD = 2
+W1_GROUPS = ((0, 1), (1, 3), (3, 5), (5, 8))
+W1_SCALE_GROUPS = ((0, 3), (3, 8))
+AHEAD = 1
 QUANT_GROUPS = ((0, 4), (4, 6), (6, 7), (7, 8))
 
 
@@ -54,7 +53,6 @@ def tile_moe_ogt_relu2_sigmoid_kernel(
         nc.gpsimd.memset(x_plane[:].rearrange("p s t -> p (s t)").bitcast(I32), 0)
         for plane in w1_planes:
             nc.vector.memset(plane[:].rearrange("p s t -> p (s t)").bitcast(I32), 0)
-        nc.vector.memset(w2_plane[:].rearrange("p s t -> p (s t)").bitcast(I32), 0)
 
         warm_in = keep.tile([P, 1], F32, name="warm_in")
         warm_out = keep.tile([P, 1], F32, name="warm_out")
@@ -63,96 +61,132 @@ def tile_moe_ogt_relu2_sigmoid_kernel(
 
         ident = keep.tile([P, P], F32, name="ident")
         make_identity(nc, ident[:])
+        nc.gpsimd.memset(w2_plane[:].rearrange("p s t -> p (s t)").bitcast(I32), 0)
 
         slot_list = keep.tile([P, SLOTS // 16], U16, name="slot_list")
         back = [keep.tile([P, T // 16], U16, name="back%d" % r) for r in range(2)]
-        nc.sync.dma_start(back[0][:], pos1)
-        xw = keep.tile([P, PASSES, T], I32, name="xw", align_bytes=64)
-        nc.sync.dma_start(out=xw[:], in_=x_words.rearrange("s p t d -> p s (t d)").bitcast(I32))
-        load_scale_rows(nc.sync, x_plane, x_scales.rearrange("s (q r) t -> r q s t", r=4))
         nc.sync.dma_start(slot_list[:], offs)
+        xw = keep.tile([P, PASSES, T], I32, name="xw", align_bytes=64)
+        load_scale_rows(nc.sync, x_plane, x_scales.rearrange("s (q r) t -> r q s t", r=4))
+        nc.sync.dma_start(out=xw[:], in_=x_words.rearrange("s p t d -> p s (t d)").bitcast(I32))
 
-        w1 = [keep.tile([P, PAIR * PASSES, 2 * H], U8, name="w1_%d" % q, align_bytes=64) for q in range(E // PAIR)]
+        w1, w1_scale = {}, {}
 
-        def load_w1(q):
-            src = w1_words[PAIR * q : PAIR * (q + 1)].rearrange("e s p b -> p (e s) b")
-            nc.sync.dma_start(out=w1[q][:].bitcast(I32), in_=src.bitcast(I32))
+        def load_w1(first, last):
+            tile = keep.tile([P, (last - first) * PASSES, 2 * H], U8, name="w1_%d" % first, align_bytes=64)
+            src = w1_words[first:last].rearrange("e s p b -> p (e s) b")
+            nc.sync.dma_start(out=tile[:].bitcast(I32), in_=src.bitcast(I32))
+            for e in range(first, last):
+                for s in range(PASSES):
+                    w1[e, s] = tile[:, (e - first) * PASSES + s, :]
 
-        w1_scale = {}
         for n, (first, last) in enumerate(W1_SCALE_GROUPS):
-            load_w1(2 * n)
+            if n == 0:
+                load_w1(*W1_GROUPS[0])
             load_scale_rows(nc.sync, w1_planes[n], w1_scales[first:last].rearrange("e s (q r) i -> r q (e s) i", r=4))
-            load_w1(2 * n + 1)
+            if n == 0:
+                load_w1(*W1_GROUPS[1])
             for e in range(first, last):
                 for s in range(PASSES):
                     w1_scale[e, s] = w1_planes[n][:, (e - first) * PASSES + s, :]
+        for group in W1_GROUPS[2:]:
+            load_w1(*group)
+        wg_raw = [keep.tile([P, PACK, N], F32, name="wg_raw%d" % s, tag="raw%d" % s, align_bytes=64) for s in range(PASSES)]
+
+        def load_wg(s):
+            nc.sync.dma_start(out=wg_raw[s][:], in_=wg[s * 512 : (s + 1) * 512, :].rearrange("(p j) n -> p j n", j=PACK))
+
+        load_wg(0)
         load_scale_rows(nc.sync, w2_plane, w2_scales.rearrange("e s (q r) i -> r q (e s) i", r=4))
         w2 = [keep.tile([P, 4, 2 * N], U8, name="w2_%d" % q, align_bytes=64) for q in range(E // 4)]
         for q in range(E // 4):
             src = w2_words[4 * q : 4 * (q + 1)].rearrange("e s p b -> p (e s) b")
             nc.sync.dma_start(out=w2[q][:].bitcast(I32), in_=src.bitcast(I32))
+        nc.sync.dma_start(back[0][:], pos1)
         nc.sync.dma_start(back[1][:], pos2)
         gates = keep.tile([P, 2, T], F32, name="gates")
         nc.sync.dma_start(out=gates[:], in_=gate.rearrange("r p t -> p r t"))
-        wg_raw = {}
-        for h in range(2):
-            for s in range(PASSES):
-                tag = {(0, 1): "stage1", (1, 1): "stage2"}.get((h, s), "wg_raw%d%d" % (h, s))
-                wg_raw[h, s] = keep.tile([P, PACK, HALF], F32, name="wg_raw%d%d" % (h, s), tag=tag, align_bytes=64)
-                src = wg[s * 512 : (s + 1) * 512, h * HALF : (h + 1) * HALF].rearrange("(p j) n -> p j n", j=PACK)
-                nc.sync.dma_start(out=wg_raw[h, s][:], in_=src)
+        load_wg(1)
+        chunks = T // P
 
-        tokens = {}
-        for first, last in GATHER_GROUPS:
-            width = (last - first) * C
-            picks = slot_list[:, first * C // 16 : last * C // 16]
+        words, scale_bytes = {}, {}
+
+        def picks(first, last):
+            return slot_list[:, first * C // 16 : last * C // 16]
+
+        def gather_bytes(first, last, tag):
             for s in range(PASSES):
-                gw = keep.tile([P, width], U32, name="gw%d%d" % (first, s), align_bytes=64)
-                gs = keep.tile([P, width], U8, name="gs%d%d" % (first, s), align_bytes=64)
-                nc.vector.tensor_copy(out=gw[:], in_=xw[:, s, :].bitcast(U32).indirect(picks))
-                nc.vector.tensor_copy(out=gs[:], in_=x_plane[:, s, :].indirect(picks))
+                tile = keep.tile([P, (last - first) * C], U8, name="gs%d%d" % (first, s), tag="%s%d" % (tag, s), align_bytes=64)
+                nc.vector.tensor_copy(out=tile[:], in_=x_plane[:, s, :].indirect(picks(first, last)))
                 for e in range(first, last):
-                    cols = slice((e - first) * C, (e - first + 1) * C)
-                    tokens[e, s] = (gw[:, cols], gs[:, cols])
+                    scale_bytes[e, s] = tile[:, (e - first) * C : (e - first + 1) * C]
+
+        def gather_words(first, last, tag, step):
+            tiles = [
+                keep.tile([P, (last - first) * C], U32, name="gw%d%d" % (first, s), tag="%s%d" % (tag, s), align_bytes=64)
+                for s in range(PASSES)
+            ]
+            for lo in range(first, last, step):
+                for s in range(PASSES):
+                    dst = tiles[s][:, (lo - first) * C : (lo - first + step) * C]
+                    nc.vector.tensor_copy(out=dst, in_=xw[:, s, :].bitcast(U32).indirect(picks(lo, lo + step)))
+            for e in range(first, last):
+                for s in range(PASSES):
+                    words[e, s] = tiles[s][:, (e - first) * C : (e - first + 1) * C]
+
+        GATHERS = {
+            0: [(gather_bytes, (0, 2, "a")), (gather_words, (0, 1, "b", 1)), (gather_words, (1, 2, "c", 1)), (gather_words, (2, 3, "d", 1))],
+            1: [(gather_bytes, (2, 4, "b"))],
+            2: [(gather_words, (3, 4, "a", 1)), (gather_bytes, (4, 6, "c"))],
+            3: [(gather_words, (4, 5, "d", 1))],
+            4: [(gather_words, (5, 7, "b", 1)), (gather_bytes, (6, 7, "a"))],
+            5: [(gather_bytes, (7, 8, "d"))],
+            6: [(gather_words, (7, 8, "c", 1))],
+        }
 
         hidden, quantised = {}, {}
         for first, last in QUANT_GROUPS:
-            tag = "stage0" if last == E else "hidden%d" % first
-            tile = keep.tile([P, last - first, C * PACK], BF16, name="hidden%d" % first, tag=tag, align_bytes=64)
+            tile = keep.tile([P, last - first, C * PACK], BF16, name="hidden%d" % first, align_bytes=64)
             for e in range(first, last):
                 hidden[e] = tile
 
+        held = {}
+
         def quantise_hidden(first, last):
-            width = (last - first) * C
-            codes = keep.tile([P, width], U32, name="h_codes%d" % first, align_bytes=64)
-            plane = keep.tile([P, width], U8, name="h_plane%d" % first, align_bytes=64)
+            base = min(first, E - 2)
+            if base not in held:
+                width = (last - first if base < E - 2 else 2) * C
+                tags = ("raw0", "stage1") if base == E - 2 else ("h_codes%d" % base, "h_plane%d" % base)
+                held[base] = (
+                    keep.tile([P, width], U32, name="h_codes%d" % base, tag=tags[0], align_bytes=64),
+                    keep.tile([P, width], U8, name="h_plane%d" % base, tag=tags[1], align_bytes=64),
+                )
+            codes, plane = held[base]
+            span = slice((first - base) * C, (last - base) * C)
             nc.vector.quantize_mx(
-                out=codes[:].bitcast(FP8X4), scales=plane[:], in_=hidden[first][:].rearrange("p e c -> p (e c)")
+                out=codes[:, span].bitcast(FP8X4), scales=plane[:, span], in_=hidden[first][:].rearrange("p e c -> p (e c)")
             )
             for e in range(first, last):
-                cols = slice((e - first) * C, (e - first + 1) * C)
+                cols = slice((e - base) * C, (e - base + 1) * C)
                 quantised[e] = (codes[:, cols], plane[:, cols])
 
         rects = {}
 
         def rectify(e):
-            pre = banks[e % 3]
+            pre = banks[e % 2]
             for s in range(PASSES):
                 nc.tensor.matmul_mx(
                     out=pre[:],
-                    lhsT=tokens[e, s][0].bitcast(FP8X4),
-                    lhsT_scale=tokens[e, s][1],
-                    rhs=w1[e // PAIR][:, (e % PAIR) * PASSES + s, :].bitcast(FP4X4),
+                    lhsT=words[e, s].bitcast(FP8X4),
+                    lhsT_scale=scale_bytes[e, s],
+                    rhs=w1[e, s].bitcast(FP4X4),
                     rhs_scale=w1_scale[e, s],
                     start=(s == 0),
                     stop=(s == PASSES - 1),
                 )
             rect = ring.tile([P, PACK, P], F32, name="rect")
             src = pre[:].rearrange("c (p t) -> c t p", t=PACK)
-            if e == E - 1:
-                nc.vector.tensor_scalar_max(out=rect[:], in0=src, scalar1=0.0)
-            else:
-                nc.scalar.activation(out=rect[:], in_=src, func=ACT.Relu)
+            nc.scalar.activation(out=rect[:], in_=src, func=ACT.Relu)
             rects[e] = rect
 
         def square(e):
@@ -167,16 +201,31 @@ def tile_moe_ogt_relu2_sigmoid_kernel(
                 func=ACT.Square,
             )
 
+        woven = {}
+
+        def weave(s, copy):
+            tile = keep.tile([P, 2, HALF * PACK], BF16, name="woven%d" % s, tag="stage%d" % s, align_bytes=64)
+            for h in range(2):
+                woven[s, h] = tile[:, h, :]
+                copy(
+                    out=woven[s, h].rearrange("p (c i j) -> p c j i", i=4, j=PACK),
+                    in_=wg_raw[s][:, :, h * HALF : (h + 1) * HALF].rearrange("p j (c i) -> p c j i", i=4),
+                )
+
         for step in range(E + AHEAD):
+            for gather, args in GATHERS.get(step, []):
+                gather(*args)
             if step < E:
                 rectify(step)
+            if step == E - 1:
+                weave(0, nc.vector.tensor_copy)
             if step >= AHEAD:
                 square(step - AHEAD)
                 for first, last in QUANT_GROUPS:
                     if last - 1 == step - AHEAD:
                         quantise_hidden(first, last)
 
-        ys = [keep.tile([P, SLOTS], F32, name="y%d" % j) for j in range(BLOCKS)]
+        ys = {}
 
         def second_layer(j, first, last, bank, on_vector):
             for e in range(first, last):
@@ -189,46 +238,41 @@ def tile_moe_ogt_relu2_sigmoid_kernel(
                     start=True,
                     stop=True,
                 )
+            if j not in ys:
+                tag = "raw1" if j == BLOCKS - 1 else "y%d" % j
+                ys[j] = keep.tile([P, SLOTS], F32, name="y%d" % j, tag=tag, align_bytes=64)
             dst, src = ys[j][:, first * C : last * C], bank[:, : (last - first) * C]
             if on_vector:
                 nc.vector.tensor_copy(out=dst, in_=src)
             else:
                 nc.scalar.copy(out=dst, in_=src)
 
-        second_layer(0, 0, 4, banks[1], True)
+        second_layer(0, 0, 4, banks[1], False)
         second_layer(0, 4, 7, banks[3], False)
         second_layer(0, 7, 8, banks[0], False)
-        second_layer(1, 0, 4, banks[4], False)
+        second_layer(1, 0, 4, banks[3], False)
         second_layer(1, 4, 8, banks[1], False)
-        second_layer(2, 0, 4, banks[3], False)
-        second_layer(2, 4, 8, banks[0], False)
+        second_layer(2, 0, 4, banks[0], False)
+        second_layer(2, 4, 8, banks[4], False)
 
         opened = [keep.tile([P, T], F32, name="o%d" % j) for j in range(BLOCKS)]
+        matrix = {}
 
-        def quantise_gate_matrix(h):
-            woven = keep.tile([P, PASSES, HALF * PACK], BF16, name="woven%d" % h, tag="stage%d" % h, align_bytes=64)
-            for s in range(PASSES):
-                nc.scalar.copy(
-                    out=woven[:, s, :].rearrange("p (c i j) -> p c j i", i=4, j=PACK),
-                    in_=wg_raw[h, s][:].rearrange("p j (c i) -> p c j i", i=4),
-                )
-            codes = keep.tile([P, PASSES, HALF], U32, name="wg_codes%d" % h, align_bytes=64)
-            planes = keep.tile([P, PASSES, HALF], U8, name="wg_plane%d" % h, align_bytes=64)
-            nc.vector.quantize_mx(
-                out=codes[:].rearrange("p s c -> p (s c)").bitcast(FP8X4),
-                scales=planes[:].rearrange("p s c -> p (s c)"),
-                in_=woven[:].rearrange("p s c -> p (s c)"),
-            )
-            return codes, planes
+        def quantise_gate_matrix(s):
+            codes = keep.tile([P, N], U32, name="wg_codes%d" % s, align_bytes=64)
+            plane = keep.tile([P, N], U8, name="wg_plane%d" % s, align_bytes=64)
+            for h in range(2):
+                cols = slice(h * HALF, (h + 1) * HALF)
+                nc.vector.quantize_mx(out=codes[:, cols].bitcast(FP8X4), scales=plane[:, cols], in_=woven[s, h])
+            matrix[s] = (codes, plane)
 
-        def output_gate(j, matrix, bank):
-            codes, planes = matrix
-            cols = slice((j % 2) * P, (j % 2 + 1) * P)
+        def output_gate(j, bank):
+            cols = slice(j * P, (j + 1) * P)
             for s in range(PASSES):
                 nc.tensor.matmul_mx(
                     out=bank[:],
-                    lhsT=codes[:, s, cols].bitcast(FP8X4),
-                    lhsT_scale=planes[:, s, cols],
+                    lhsT=matrix[s][0][:, cols].bitcast(FP8X4),
+                    lhsT_scale=matrix[s][1][:, cols],
                     rhs=xw[:, s, :].bitcast(FP8X4),
                     rhs_scale=x_plane[:, s, :],
                     start=(s == 0),
@@ -236,52 +280,56 @@ def tile_moe_ogt_relu2_sigmoid_kernel(
                 )
             nc.scalar.activation(out=opened[j][:], in_=bank[:], func=ACT.Sigmoid)
 
-        def fetch(j, first_tag):
-            parts = []
-            for r in range(2):
-                tag = first_tag if r == 0 else "second%d" % j
-                part = keep.tile([P, T], F32, name="part%d%d" % (j, r), tag=tag, align_bytes=64)
-                nc.vector.tensor_tensor(part[:], ys[j][:].indirect(back[r][:]), gates[:, r, :], ALU.mult)
-                parts.append(part)
-            return parts
+        parts = {}
 
-        def add_on_vector(j, parts):
-            total = keep.tile([P, T], F32, name="sum%d" % j)
-            nc.vector.tensor_tensor(total[:], parts[0][:], parts[1][:], ALU.add)
-            return total
+        def fetch(j, r, part):
+            nc.vector.tensor_tensor(part, ys[j][:].indirect(back[r][:]), gates[:, r, :], ALU.mult)
+            parts[j, r] = part
 
-        def add_turned(parts, bank):
-            for c in range(T // P):
+        def add_turned(j, bank):
+            for c in range(chunks):
                 cols = slice(c * P, (c + 1) * P)
                 for r in range(2):
-                    nc.tensor.matmul(bank[:, cols], parts[r][:, cols], ident[:], start=(r == 0), stop=(r == 1), is_transpose=True)
+                    nc.tensor.matmul(bank[:, cols], parts[j, r][:, cols], ident[:], start=(r == 0), stop=(r == 1), is_transpose=True)
 
         def turn_back(staged, bank):
             nc.scalar.copy(out=staged, in_=bank[:])
-            for c in range(T // P):
+            for c in range(chunks):
                 cols = slice(c * P, (c + 1) * P)
                 nc.tensor.transpose(bank[:, cols], staged[:, cols], ident[:])
-            return bank
 
         def finish(j, total):
             res = keep.tile([P, T], F32, name="res%d" % j)
             nc.vector.tensor_tensor(res[:], total[:], opened[j][:], ALU.mult)
             nc.sync.dma_start(out=out[j * P : (j + 1) * P, :], in_=res[:])
 
-        totals = {}
-        for j in range(2):
-            add_turned(fetch(j, "first%d" % j), banks[6 + j])
-        low = quantise_gate_matrix(0)
-        parts = fetch(2, "stage0")
-        high = quantise_gate_matrix(1)
-        totals[2] = add_on_vector(2, parts)
-        second_layer(3, 0, 4, banks[4], False)
+        sums = [banks[b] for b in (6, 7, 2)]
+        quantise_gate_matrix(0)
+        early = keep.tile([P, 4, T], F32, name="early", tag="stage0", align_bytes=64)
+        fetch(0, 0, early[:, 0, :])
+        fetch(0, 1, early[:, 1, :])
+        weave(1, nc.scalar.copy)
+        second_layer(3, 0, 4, banks[3], False)
         second_layer(3, 4, 8, banks[1], False)
-        totals[3] = add_on_vector(3, fetch(3, "stage1"))
-        staged = keep.tile([P, 2, T], F32, name="staged", tag="stage2", align_bytes=64)
-        for j in range(2):
-            totals[j] = turn_back(staged[:, j, :], banks[6 + j])
-        for j, bank in enumerate((2, 5, 3, 0)):
-            output_gate(j, (low, high)[j // 2], banks[bank])
+        add_turned(0, sums[0])
+        fetch(1, 0, early[:, 2, :])
+        fetch(1, 1, early[:, 3, :])
+        add_turned(1, sums[1])
+        quantise_gate_matrix(1)
+        late = keep.tile([P, 7, T], F32, name="late", tag="stage1", align_bytes=64)
+        staged = late[:, 4:7, :]
+        fetch(2, 0, late[:, 0, :])
+        fetch(2, 1, late[:, 1, :])
+        turn_back(staged[:, 0, :], sums[0])
+        for j, b in enumerate((5, 0, 4, 3)):
+            output_gate(j, banks[b])
+        turn_back(staged[:, 1, :], sums[1])
+        add_turned(2, sums[2])
+        turn_back(staged[:, 2, :], sums[2])
+        fetch(3, 0, late[:, 2, :])
+        fetch(3, 1, late[:, 3, :])
+        last = keep.tile([P, T], F32, name="last")
+        nc.vector.tensor_tensor(last[:], parts[3, 0], parts[3, 1], ALU.add)
+        sums.append(last)
         for j in range(BLOCKS):
-            finish(j, totals[j])
+            finish(j, sums[j])

@@ -25,7 +25,7 @@ BLOCKS = N // P
 HALF = N // 2
 W1_GROUPS = ((0, 1), (1, 3), (3, 5), (5, 8))
 W1_SCALE_GROUPS = ((0, 3), (3, 8))
-AHEAD = 1
+AHEAD = 2
 QUANT_GROUPS = ((0, 4), (4, 6), (6, 7), (7, 8))
 
 
@@ -96,12 +96,12 @@ def tile_moe_ogt_relu2_sigmoid_kernel(
         def load_wg(s):
             nc.sync.dma_start(out=wg_raw[s][:], in_=wg[s * 512 : (s + 1) * 512, :].rearrange("(p j) n -> p j n", j=PACK))
 
-        load_wg(0)
         load_scale_rows(nc.sync, w2_plane, w2_scales.rearrange("e s (q r) i -> r q (e s) i", r=4))
         w2 = [keep.tile([P, 4, 2 * N], U8, name="w2_%d" % q, align_bytes=64) for q in range(E // 4)]
         for q in range(E // 4):
             src = w2_words[4 * q : 4 * (q + 1)].rearrange("e s p b -> p (e s) b")
             nc.sync.dma_start(out=w2[q][:].bitcast(I32), in_=src.bitcast(I32))
+        load_wg(0)
         nc.sync.dma_start(back[0][:], pos1)
         nc.sync.dma_start(back[1][:], pos2)
         gates = keep.tile([P, 2, T], F32, name="gates")
@@ -156,7 +156,7 @@ def tile_moe_ogt_relu2_sigmoid_kernel(
             base = min(first, E - 2)
             if base not in held:
                 width = (last - first if base < E - 2 else 2) * C
-                tags = ("raw0", "stage1") if base == E - 2 else ("h_codes%d" % base, "h_plane%d" % base)
+                tags = ("h_codes%d" % base, "h_plane%d" % base)
                 held[base] = (
                     keep.tile([P, width], U32, name="h_codes%d" % base, tag=tags[0], align_bytes=64),
                     keep.tile([P, width], U8, name="h_plane%d" % base, tag=tags[1], align_bytes=64),
@@ -173,7 +173,7 @@ def tile_moe_ogt_relu2_sigmoid_kernel(
         rects = {}
 
         def rectify(e):
-            pre = banks[e % 2]
+            pre = banks[e % 3]
             for s in range(PASSES):
                 nc.tensor.matmul_mx(
                     out=pre[:],
@@ -186,7 +186,10 @@ def tile_moe_ogt_relu2_sigmoid_kernel(
                 )
             rect = ring.tile([P, PACK, P], F32, name="rect")
             src = pre[:].rearrange("c (p t) -> c t p", t=PACK)
-            nc.scalar.activation(out=rect[:], in_=src, func=ACT.Relu)
+            if e == E - 1:
+                nc.vector.tensor_scalar_max(out=rect[:], in0=src, scalar1=0.0)
+            else:
+                nc.scalar.activation(out=rect[:], in_=src, func=ACT.Relu)
             rects[e] = rect
 
         def square(e):
@@ -203,22 +206,24 @@ def tile_moe_ogt_relu2_sigmoid_kernel(
 
         woven = {}
 
-        def weave(s, copy):
-            tile = keep.tile([P, 2, HALF * PACK], BF16, name="woven%d" % s, tag="stage%d" % s, align_bytes=64)
+        def weave(s):
             for h in range(2):
-                woven[s, h] = tile[:, h, :]
-                copy(
-                    out=woven[s, h].rearrange("p (c i j) -> p c j i", i=4, j=PACK),
-                    in_=wg_raw[s][:, :, h * HALF : (h + 1) * HALF].rearrange("p j (c i) -> p c j i", i=4),
-                )
+                tile = keep.tile([P, HALF * PACK], BF16, name="woven%d%d" % (s, h), tag="stage%d%d" % (s, h), align_bytes=64)
+                woven[s, h] = tile[:]
+                src = wg_raw[s][:, :, h * HALF : (h + 1) * HALF]
+                if s == 0:
+                    nc.vector.tensor_copy(out=woven[s, h].rearrange("p (c j) -> p c j", j=PACK), in_=src.rearrange("p j c -> p c j"))
+                else:
+                    nc.scalar.copy(
+                        out=woven[s, h].rearrange("p (c i j) -> p c j i", i=4, j=PACK),
+                        in_=src.rearrange("p j (c i) -> p c j i", i=4),
+                    )
 
         for step in range(E + AHEAD):
             for gather, args in GATHERS.get(step, []):
                 gather(*args)
             if step < E:
                 rectify(step)
-            if step == E - 1:
-                weave(0, nc.vector.tensor_copy)
             if step >= AHEAD:
                 square(step - AHEAD)
                 for first, last in QUANT_GROUPS:
@@ -266,70 +271,73 @@ def tile_moe_ogt_relu2_sigmoid_kernel(
                 nc.vector.quantize_mx(out=codes[:, cols].bitcast(FP8X4), scales=plane[:, cols], in_=woven[s, h])
             matrix[s] = (codes, plane)
 
-        def output_gate(j, bank):
+        gate_banks = [banks[b] for b in (5, 2, 0, 4)]
+
+        def gate_pass(j, s):
             cols = slice(j * P, (j + 1) * P)
-            for s in range(PASSES):
-                nc.tensor.matmul_mx(
-                    out=bank[:],
-                    lhsT=matrix[s][0][:, cols].bitcast(FP8X4),
-                    lhsT_scale=matrix[s][1][:, cols],
-                    rhs=xw[:, s, :].bitcast(FP8X4),
-                    rhs_scale=x_plane[:, s, :],
-                    start=(s == 0),
-                    stop=(s == PASSES - 1),
-                )
-            nc.scalar.activation(out=opened[j][:], in_=bank[:], func=ACT.Sigmoid)
+            nc.tensor.matmul_mx(
+                out=gate_banks[j][:],
+                lhsT=matrix[s][0][:, cols].bitcast(FP8X4),
+                lhsT_scale=matrix[s][1][:, cols],
+                rhs=xw[:, s, :].bitcast(FP8X4),
+                rhs_scale=x_plane[:, s, :],
+                start=(s == 0),
+                stop=(s == PASSES - 1),
+            )
 
-        parts = {}
+        def fetch(j, r, part, first=0, last=T):
+            window = ys[j][:].indirect(back[r][:, first // 16 : last // 16])
+            nc.vector.tensor_tensor(part[:, first:last], window, gates[:, r, first:last], ALU.mult)
 
-        def fetch(j, r, part):
-            nc.vector.tensor_tensor(part, ys[j][:].indirect(back[r][:]), gates[:, r, :], ALU.mult)
-            parts[j, r] = part
-
-        def add_turned(j, bank):
-            for c in range(chunks):
-                cols = slice(c * P, (c + 1) * P)
+        def add_turned(parts, bank, first=0, last=T):
+            for c in range(first, last, P):
                 for r in range(2):
-                    nc.tensor.matmul(bank[:, cols], parts[j, r][:, cols], ident[:], start=(r == 0), stop=(r == 1), is_transpose=True)
+                    nc.tensor.matmul(bank[:, c : c + P], parts[:, r, c : c + P], ident[:], start=(r == 0), stop=(r == 1), is_transpose=True)
 
-        def turn_back(staged, bank):
-            nc.scalar.copy(out=staged, in_=bank[:])
-            for c in range(chunks):
-                cols = slice(c * P, (c + 1) * P)
-                nc.tensor.transpose(bank[:, cols], staged[:, cols], ident[:])
+        def turn_back(staged, bank, first=0, last=T):
+            nc.scalar.copy(out=staged[:, first:last], in_=bank[:, first:last])
+            for c in range(first, last, P):
+                nc.tensor.transpose(bank[:, c : c + P], staged[:, c : c + P], ident[:])
 
-        def finish(j, total):
-            res = keep.tile([P, T], F32, name="res%d" % j)
-            nc.vector.tensor_tensor(res[:], total[:], opened[j][:], ALU.mult)
-            nc.sync.dma_start(out=out[j * P : (j + 1) * P, :], in_=res[:])
+        def finish(j, bank, first=0, last=T):
+            res = keep.tile([P, last - first], F32, name="res%d%d" % (j, first))
+            nc.vector.tensor_tensor(res[:], bank[:, first:last], opened[j][:, first:last], ALU.mult)
+            nc.sync.dma_start(out=out[j * P : (j + 1) * P, first:last], in_=res[:])
 
-        sums = [banks[b] for b in (6, 7, 2)]
+        sums = [banks[b] for b in (6, 7, 3)]
+        weave(0)
         quantise_gate_matrix(0)
-        early = keep.tile([P, 4, T], F32, name="early", tag="stage0", align_bytes=64)
+        early = keep.tile([P, 4, T], F32, name="early", tag="stage00", align_bytes=64)
         fetch(0, 0, early[:, 0, :])
         fetch(0, 1, early[:, 1, :])
-        weave(1, nc.scalar.copy)
+        weave(1)
         second_layer(3, 0, 4, banks[3], False)
         second_layer(3, 4, 8, banks[1], False)
-        add_turned(0, sums[0])
+        for j in range(BLOCKS):
+            gate_pass(j, 0)
+        add_turned(early[:, 0:2, :], sums[0])
         fetch(1, 0, early[:, 2, :])
         fetch(1, 1, early[:, 3, :])
-        add_turned(1, sums[1])
+        add_turned(early[:, 2:4, :], sums[1])
         quantise_gate_matrix(1)
-        late = keep.tile([P, 7, T], F32, name="late", tag="stage1", align_bytes=64)
-        staged = late[:, 4:7, :]
+        late = keep.tile([P, 4, T], F32, name="late", tag="stage11", align_bytes=64)
+        staged = keep.tile([P, 4, T], F32, name="staged", tag="stage10", align_bytes=64)
         fetch(2, 0, late[:, 0, :])
         fetch(2, 1, late[:, 1, :])
         turn_back(staged[:, 0, :], sums[0])
-        for j, b in enumerate((5, 0, 4, 3)):
-            output_gate(j, banks[b])
-        turn_back(staged[:, 1, :], sums[1])
-        add_turned(2, sums[2])
-        turn_back(staged[:, 2, :], sums[2])
-        fetch(3, 0, late[:, 2, :])
-        fetch(3, 1, late[:, 3, :])
-        last = keep.tile([P, T], F32, name="last")
-        nc.vector.tensor_tensor(last[:], parts[3, 0], parts[3, 1], ALU.add)
-        sums.append(last)
         for j in range(BLOCKS):
+            gate_pass(j, 1)
+            nc.scalar.activation(out=opened[j][:], in_=gate_banks[j][:], func=ACT.Sigmoid)
+        turn_back(staged[:, 1, :], sums[1])
+        add_turned(late[:, 0:2, :], sums[2])
+        turn_back(staged[:, 2, :], sums[2])
+        halves = ((0, T // 2, banks[1]), (T // 2, T, banks[5]))
+        fetch(3, 0, late[:, 2, :])
+        for first, last, bank in halves:
+            fetch(3, 1, late[:, 3, :], first, last)
+            add_turned(late[:, 2:4, :], bank, first, last)
+            turn_back(staged[:, 3, :], bank, first, last)
+        for j in range(BLOCKS - 1):
             finish(j, sums[j])
+        for first, last, bank in halves:
+            finish(3, bank, first, last)

@@ -23,8 +23,9 @@ PASSES = K // (P * PACK)
 SLOTS = E * C
 BLOCKS = N // P
 HALF = N // 2
-W1_GROUPS = ((0, 1), (1, 3), (3, 5), (5, 8))
-W1_SCALE_GROUPS = ((0, 3), (3, 8))
+GATHER_GROUPS = ((0, 2), (2, 4), (4, 6), (6, 7), (7, 8))
+W1_GROUPS = ((0, 2), (2, 4), (4, 6), (6, 8))
+W1_SCALE_GROUPS = ((0, 4), (4, 8))
 AHEAD = 2
 QUANT_GROUPS = ((0, 4), (4, 6), (6, 7), (7, 8))
 
@@ -65,10 +66,11 @@ def tile_moe_ogt_relu2_sigmoid_kernel(
 
         slot_list = keep.tile([P, SLOTS // 16], U16, name="slot_list")
         back = [keep.tile([P, T // 16], U16, name="back%d" % r) for r in range(2)]
-        nc.sync.dma_start(slot_list[:], offs)
+        nc.sync.dma_start(back[0][:], pos1)
         xw = keep.tile([P, PASSES, T], I32, name="xw", align_bytes=64)
-        load_scale_rows(nc.sync, x_plane, x_scales.rearrange("s (q r) t -> r q s t", r=4))
         nc.sync.dma_start(out=xw[:], in_=x_words.rearrange("s p t d -> p s (t d)").bitcast(I32))
+        load_scale_rows(nc.sync, x_plane, x_scales.rearrange("s (q r) t -> r q s t", r=4))
+        nc.sync.dma_start(slot_list[:], offs)
 
         w1, w1_scale = {}, {}
 
@@ -81,32 +83,30 @@ def tile_moe_ogt_relu2_sigmoid_kernel(
                     w1[e, s] = tile[:, (e - first) * PASSES + s, :]
 
         for n, (first, last) in enumerate(W1_SCALE_GROUPS):
-            if n == 0:
-                load_w1(*W1_GROUPS[0])
+            load_w1(*W1_GROUPS[2 * n])
             load_scale_rows(nc.sync, w1_planes[n], w1_scales[first:last].rearrange("e s (q r) i -> r q (e s) i", r=4))
-            if n == 0:
-                load_w1(*W1_GROUPS[1])
+            load_w1(*W1_GROUPS[2 * n + 1])
             for e in range(first, last):
                 for s in range(PASSES):
                     w1_scale[e, s] = w1_planes[n][:, (e - first) * PASSES + s, :]
-        for group in W1_GROUPS[2:]:
-            load_w1(*group)
-        wg_raw = [keep.tile([P, PACK, N], F32, name="wg_raw%d" % s, tag="raw%d" % s, align_bytes=64) for s in range(PASSES)]
+        wg_raw = {}
 
-        def load_wg(s):
-            nc.sync.dma_start(out=wg_raw[s][:], in_=wg[s * 512 : (s + 1) * 512, :].rearrange("(p j) n -> p j n", j=PACK))
+        def load_wg(s, first, last):
+            tile = keep.tile([P, PACK, last - first], F32, name="wg_raw%d%d" % (s, first), tag="raw%d%d" % (s, first), align_bytes=64)
+            nc.sync.dma_start(out=tile[:], in_=wg[s * 512 : (s + 1) * 512, first:last].rearrange("(p j) n -> p j n", j=PACK))
+            for h in range(first // HALF, last // HALF):
+                wg_raw[s, h] = tile[:, :, h * HALF - first : (h + 1) * HALF - first]
 
         load_scale_rows(nc.sync, w2_plane, w2_scales.rearrange("e s (q r) i -> r q (e s) i", r=4))
         w2 = [keep.tile([P, 4, 2 * N], U8, name="w2_%d" % q, align_bytes=64) for q in range(E // 4)]
         for q in range(E // 4):
             src = w2_words[4 * q : 4 * (q + 1)].rearrange("e s p b -> p (e s) b")
             nc.sync.dma_start(out=w2[q][:].bitcast(I32), in_=src.bitcast(I32))
-        load_wg(0)
-        nc.sync.dma_start(back[0][:], pos1)
+            load_wg(0, q * HALF, (q + 1) * HALF)
         nc.sync.dma_start(back[1][:], pos2)
         gates = keep.tile([P, 2, T], F32, name="gates")
         nc.sync.dma_start(out=gates[:], in_=gate.rearrange("r p t -> p r t"))
-        load_wg(1)
+        load_wg(1, 0, N)
         chunks = T // P
 
         words, scale_bytes = {}, {}
@@ -114,35 +114,16 @@ def tile_moe_ogt_relu2_sigmoid_kernel(
         def picks(first, last):
             return slot_list[:, first * C // 16 : last * C // 16]
 
-        def gather_bytes(first, last, tag):
+        for first, last in GATHER_GROUPS:
+            width = (last - first) * C
             for s in range(PASSES):
-                tile = keep.tile([P, (last - first) * C], U8, name="gs%d%d" % (first, s), tag="%s%d" % (tag, s), align_bytes=64)
-                nc.vector.tensor_copy(out=tile[:], in_=x_plane[:, s, :].indirect(picks(first, last)))
+                gw = keep.tile([P, width], U32, name="gw%d%d" % (first, s), align_bytes=64)
+                gs = keep.tile([P, width], U8, name="gs%d%d" % (first, s), align_bytes=64)
+                nc.vector.tensor_copy(out=gw[:], in_=xw[:, s, :].bitcast(U32).indirect(picks(first, last)))
+                nc.vector.tensor_copy(out=gs[:], in_=x_plane[:, s, :].indirect(picks(first, last)))
                 for e in range(first, last):
-                    scale_bytes[e, s] = tile[:, (e - first) * C : (e - first + 1) * C]
-
-        def gather_words(first, last, tag, step):
-            tiles = [
-                keep.tile([P, (last - first) * C], U32, name="gw%d%d" % (first, s), tag="%s%d" % (tag, s), align_bytes=64)
-                for s in range(PASSES)
-            ]
-            for lo in range(first, last, step):
-                for s in range(PASSES):
-                    dst = tiles[s][:, (lo - first) * C : (lo - first + step) * C]
-                    nc.vector.tensor_copy(out=dst, in_=xw[:, s, :].bitcast(U32).indirect(picks(lo, lo + step)))
-            for e in range(first, last):
-                for s in range(PASSES):
-                    words[e, s] = tiles[s][:, (e - first) * C : (e - first + 1) * C]
-
-        GATHERS = {
-            0: [(gather_bytes, (0, 2, "a")), (gather_words, (0, 1, "b", 1)), (gather_words, (1, 2, "c", 1)), (gather_words, (2, 3, "d", 1))],
-            1: [(gather_bytes, (2, 4, "b"))],
-            2: [(gather_words, (3, 4, "a", 1)), (gather_bytes, (4, 6, "c"))],
-            3: [(gather_words, (4, 5, "d", 1))],
-            4: [(gather_words, (5, 7, "b", 1)), (gather_bytes, (6, 7, "a"))],
-            5: [(gather_bytes, (7, 8, "d"))],
-            6: [(gather_words, (7, 8, "c", 1))],
-        }
+                    words[e, s] = gw[:, (e - first) * C : (e - first + 1) * C]
+                    scale_bytes[e, s] = gs[:, (e - first) * C : (e - first + 1) * C]
 
         hidden, quantised = {}, {}
         for first, last in QUANT_GROUPS:
@@ -156,7 +137,7 @@ def tile_moe_ogt_relu2_sigmoid_kernel(
             base = min(first, E - 2)
             if base not in held:
                 width = (last - first if base < E - 2 else 2) * C
-                tags = ("h_codes%d" % base, "h_plane%d" % base)
+                tags = ("raw00" if base == E - 2 else "h_codes%d" % base, "h_plane%d" % base)
                 held[base] = (
                     keep.tile([P, width], U32, name="h_codes%d" % base, tag=tags[0], align_bytes=64),
                     keep.tile([P, width], U8, name="h_plane%d" % base, tag=tags[1], align_bytes=64),
@@ -184,7 +165,10 @@ def tile_moe_ogt_relu2_sigmoid_kernel(
                     start=(s == 0),
                     stop=(s == PASSES - 1),
                 )
-            rect = ring.tile([P, PACK, P], F32, name="rect")
+            if e == E - 1:
+                rect = keep.tile([P, PACK, P], F32, name="rect_last", tag="stage00", align_bytes=64)
+            else:
+                rect = ring.tile([P, PACK, P], F32, name="rect")
             src = pre[:].rearrange("c (p t) -> c t p", t=PACK)
             if e == E - 1:
                 nc.vector.tensor_scalar_max(out=rect[:], in0=src, scalar1=0.0)
@@ -206,28 +190,27 @@ def tile_moe_ogt_relu2_sigmoid_kernel(
 
         woven = {}
 
-        def weave(s):
-            for h in range(2):
-                tile = keep.tile([P, HALF * PACK], BF16, name="woven%d%d" % (s, h), tag="stage%d%d" % (s, h), align_bytes=64)
-                woven[s, h] = tile[:]
-                src = wg_raw[s][:, :, h * HALF : (h + 1) * HALF]
-                if s == 0:
-                    nc.vector.tensor_copy(out=woven[s, h].rearrange("p (c j) -> p c j", j=PACK), in_=src.rearrange("p j c -> p c j"))
-                else:
-                    nc.scalar.copy(
-                        out=woven[s, h].rearrange("p (c i j) -> p c j i", i=4, j=PACK),
-                        in_=src.rearrange("p j (c i) -> p c j i", i=4),
-                    )
+        def weave(s, h):
+            tile = keep.tile([P, HALF * PACK], BF16, name="woven%d%d" % (s, h), tag="stage%d%d" % (s, h), align_bytes=64)
+            woven[s, h] = tile[:]
+            if s == 0:
+                nc.vector.tensor_copy(out=tile[:].rearrange("p (c j) -> p c j", j=PACK), in_=wg_raw[s, h].rearrange("p j c -> p c j"))
+            else:
+                nc.scalar.copy(
+                    out=tile[:].rearrange("p (c i j) -> p c j i", i=4, j=PACK),
+                    in_=wg_raw[s, h].rearrange("p j (c i) -> p c j i", i=4),
+                )
 
         for step in range(E + AHEAD):
-            for gather, args in GATHERS.get(step, []):
-                gather(*args)
             if step < E:
                 rectify(step)
             if step >= AHEAD:
                 square(step - AHEAD)
+                if step - AHEAD == E - 1:
+                    weave(0, 0)
+                    quantise_hidden(E - 2, E - 1)
                 for first, last in QUANT_GROUPS:
-                    if last - 1 == step - AHEAD:
+                    if last - 1 == step - AHEAD and first != E - 2:
                         quantise_hidden(first, last)
 
         ys = {}
@@ -244,7 +227,7 @@ def tile_moe_ogt_relu2_sigmoid_kernel(
                     stop=True,
                 )
             if j not in ys:
-                tag = "raw1" if j == BLOCKS - 1 else "y%d" % j
+                tag = "raw10" if j == BLOCKS - 1 else "y%d" % j
                 ys[j] = keep.tile([P, SLOTS], F32, name="y%d" % j, tag=tag, align_bytes=64)
             dst, src = ys[j][:, first * C : last * C], bank[:, : (last - first) * C]
             if on_vector:
@@ -305,12 +288,13 @@ def tile_moe_ogt_relu2_sigmoid_kernel(
             nc.sync.dma_start(out=out[j * P : (j + 1) * P, first:last], in_=res[:])
 
         sums = [banks[b] for b in (6, 7, 3)]
-        weave(0)
+        weave(0, 1)
         quantise_gate_matrix(0)
-        early = keep.tile([P, 4, T], F32, name="early", tag="stage00", align_bytes=64)
+        early = keep.tile([P, 4, T], F32, name="early", tag="stage01", align_bytes=64)
         fetch(0, 0, early[:, 0, :])
         fetch(0, 1, early[:, 1, :])
-        weave(1)
+        weave(1, 0)
+        weave(1, 1)
         second_layer(3, 0, 4, banks[3], False)
         second_layer(3, 4, 8, banks[1], False)
         for j in range(BLOCKS):

@@ -19,20 +19,26 @@ ALU = mybir.AluOpType
 
 P = 128
 PACK = 4
-PASSES = K // (P * PACK)
+K_PASS = P * PACK
+PASSES = K // K_PASS
 SLOTS = E * C
 BLOCKS = N // P
+CHUNKS = T // P
 HALF = N // 2
+BANK = 512
+PER_BANK = BANK // C
+STRIPE = 16
 GATHER_GROUPS = ((0, 2), (2, 4), (4, 6), (6, 7), (7, 8))
 W1_GROUPS = ((0, 2), (2, 4), (4, 6), (6, 8))
 W1_SCALE_GROUPS = ((0, 4), (4, 8))
-AHEAD = 2
 QUANT_GROUPS = ((0, 4), (4, 6), (6, 7), (7, 8))
+AHEAD = 2
+DEPTH = AHEAD + 1
 
 
-def load_scale_rows(queue, plane, rows):
+def load_scale_rows(nc, plane, rows):
     for r in range(4):
-        queue.dma_start(out=plane[r:P:32, :, :].bitcast(I32), in_=rows[r].bitcast(I32))
+        nc.sync.dma_start(out=plane[r:P:32, :, :].bitcast(I32), in_=rows[r].bitcast(I32))
 
 
 def tile_moe_ogt_relu2_sigmoid_kernel(
@@ -41,9 +47,9 @@ def tile_moe_ogt_relu2_sigmoid_kernel(
     nc = tc.nc
     with ExitStack() as ctx:
         keep = ctx.enter_context(tc.tile_pool(name="keep", bufs=1))
-        ring = ctx.enter_context(tc.tile_pool(name="ring", bufs=3))
+        ring = ctx.enter_context(tc.tile_pool(name="ring", bufs=DEPTH))
         psum = ctx.enter_context(tc.psum_pool(name="psum", bufs=1))
-        banks = [psum.tile([P, 512], F32, name="bank%d" % b) for b in range(8)]
+        banks = [psum.tile([P, BANK], F32, name="bank%d" % b) for b in range(8)]
 
         x_plane = keep.tile([P, PASSES, T], U8, name="x_plane", align_bytes=64)
         w1_planes = [
@@ -51,25 +57,23 @@ def tile_moe_ogt_relu2_sigmoid_kernel(
             for first, last in W1_SCALE_GROUPS
         ]
         w2_plane = keep.tile([P, E, N], U8, name="w2_plane", align_bytes=64)
+        gate_rows = keep.tile([P, P], F32, name="gate_rows")
+        nc.gpsimd.memset(gate_rows[:], 0.0)
         nc.gpsimd.memset(x_plane[:].rearrange("p s t -> p (s t)").bitcast(I32), 0)
         for plane in w1_planes:
             nc.vector.memset(plane[:].rearrange("p s t -> p (s t)").bitcast(I32), 0)
-
-        warm_in = keep.tile([P, 1], F32, name="warm_in")
-        warm_out = keep.tile([P, 1], F32, name="warm_out")
-        nc.gpsimd.memset(warm_in[:], 0.0)
-        nc.scalar.activation(out=warm_out[:], in_=warm_in[:], func=ACT.Sigmoid)
 
         ident = keep.tile([P, P], F32, name="ident")
         make_identity(nc, ident[:])
         nc.gpsimd.memset(w2_plane[:].rearrange("p s t -> p (s t)").bitcast(I32), 0)
 
-        slot_list = keep.tile([P, SLOTS // 16], U16, name="slot_list")
-        back = [keep.tile([P, T // 16], U16, name="back%d" % r) for r in range(2)]
-        nc.sync.dma_start(back[0][:], pos1)
+        slot_list = keep.tile([P, SLOTS // STRIPE], U16, name="slot_list")
+        back = [keep.tile([P, T // STRIPE], U16, name="back%d" % r) for r in range(2)]
         xw = keep.tile([P, PASSES, T], I32, name="xw", align_bytes=64)
         nc.sync.dma_start(out=xw[:], in_=x_words.rearrange("s p t d -> p s (t d)").bitcast(I32))
-        load_scale_rows(nc.sync, x_plane, x_scales.rearrange("s (q r) t -> r q s t", r=4))
+        gate_runs = gate.rearrange("r p (c t) -> (r p c) t", t=P)
+        nc.sync.dma_start(out=gate_rows[0 : 2 * CHUNKS, :], in_=gate_runs[0 : 2 * P * CHUNKS : P + 1, :])
+        load_scale_rows(nc, x_plane, x_scales.rearrange("s (q r) t -> r q s t", r=4))
         nc.sync.dma_start(slot_list[:], offs)
 
         w1, w1_scale = {}, {}
@@ -82,67 +86,72 @@ def tile_moe_ogt_relu2_sigmoid_kernel(
                 for s in range(PASSES):
                     w1[e, s] = tile[:, (e - first) * PASSES + s, :]
 
-        for n, (first, last) in enumerate(W1_SCALE_GROUPS):
-            load_w1(*W1_GROUPS[2 * n])
-            load_scale_rows(nc.sync, w1_planes[n], w1_scales[first:last].rearrange("e s (q r) i -> r q (e s) i", r=4))
-            load_w1(*W1_GROUPS[2 * n + 1])
+        for run, (first, last) in enumerate(W1_SCALE_GROUPS):
+            load_w1(*W1_GROUPS[2 * run])
+            load_scale_rows(nc, w1_planes[run], w1_scales[first:last].rearrange("e s (q r) i -> r q (e s) i", r=4))
+            load_w1(*W1_GROUPS[2 * run + 1])
             for e in range(first, last):
                 for s in range(PASSES):
-                    w1_scale[e, s] = w1_planes[n][:, (e - first) * PASSES + s, :]
+                    w1_scale[e, s] = w1_planes[run][:, (e - first) * PASSES + s, :]
+
         wg_raw = {}
 
         def load_wg(s, first, last):
-            tile = keep.tile([P, PACK, last - first], F32, name="wg_raw%d%d" % (s, first), tag="raw%d%d" % (s, first), align_bytes=64)
-            nc.sync.dma_start(out=tile[:], in_=wg[s * 512 : (s + 1) * 512, first:last].rearrange("(p j) n -> p j n", j=PACK))
-            for h in range(first // HALF, last // HALF):
-                wg_raw[s, h] = tile[:, :, h * HALF - first : (h + 1) * HALF - first]
+            tile = keep.tile(
+                [P, PACK, last - first], F32, name="wg_raw%d%d" % (s, first), tag="raw%d%d" % (s, first // HALF), align_bytes=64
+            )
+            src = wg[s * K_PASS : (s + 1) * K_PASS, first:last].rearrange("(p d) n -> p d n", d=PACK)
+            nc.sync.dma_start(out=tile[:], in_=src)
+            for half in range(first // HALF, last // HALF):
+                wg_raw[s, half] = tile[:, :, half * HALF - first : (half + 1) * HALF - first]
 
-        load_scale_rows(nc.sync, w2_plane, w2_scales.rearrange("e s (q r) i -> r q (e s) i", r=4))
-        w2 = [keep.tile([P, 4, 2 * N], U8, name="w2_%d" % q, align_bytes=64) for q in range(E // 4)]
-        for q in range(E // 4):
-            src = w2_words[4 * q : 4 * (q + 1)].rearrange("e s p b -> p (e s) b")
-            nc.sync.dma_start(out=w2[q][:].bitcast(I32), in_=src.bitcast(I32))
-            load_wg(0, q * HALF, (q + 1) * HALF)
+        load_scale_rows(nc, w2_plane, w2_scales.rearrange("e s (q r) n -> r q (e s) n", r=4))
+        w2 = [keep.tile([P, PER_BANK, 2 * N], U8, name="w2_%d" % q, align_bytes=64) for q in range(E // PER_BANK)]
+        load_wg(0, 0, HALF)
+        for q, tile in enumerate(w2):
+            src = w2_words[PER_BANK * q : PER_BANK * (q + 1)].rearrange("e s p b -> p (e s) b")
+            nc.sync.dma_start(out=tile[:].bitcast(I32), in_=src.bitcast(I32))
+        load_wg(0, HALF, N)
+        nc.sync.dma_start(back[0][:], pos1)
         nc.sync.dma_start(back[1][:], pos2)
-        gates = keep.tile([P, 2, T], F32, name="gates")
-        nc.sync.dma_start(out=gates[:], in_=gate.rearrange("r p t -> p r t"))
         load_wg(1, 0, N)
-        chunks = T // P
+
+        gate_cols = keep.tile([P, 2 * CHUNKS], F32, name="gate_cols")
+        nc.tensor.transpose(banks[5][:, 0:P], gate_rows[:], ident[:])
+        nc.scalar.copy(out=gate_cols[:], in_=banks[5][:, 0 : 2 * CHUNKS])
+        gates = keep.tile([P, 2, T], F32, name="gates")
+        for r in range(2):
+            for c in range(CHUNKS):
+                column = gate_cols[:, r * CHUNKS + c : r * CHUNKS + c + 1]
+                nc.tensor.transpose(banks[6 + r][:, c * P : (c + 1) * P], column.to_broadcast([P, P]), ident[:])
+            nc.scalar.copy(out=gates[:, r, :], in_=banks[6 + r][:])
 
         words, scale_bytes = {}, {}
-
-        def picks(first, last):
-            return slot_list[:, first * C // 16 : last * C // 16]
-
         for first, last in GATHER_GROUPS:
             width = (last - first) * C
+            picks = slot_list[:, first * C // STRIPE : last * C // STRIPE]
             for s in range(PASSES):
                 gw = keep.tile([P, width], U32, name="gw%d%d" % (first, s), align_bytes=64)
                 gs = keep.tile([P, width], U8, name="gs%d%d" % (first, s), align_bytes=64)
-                nc.vector.tensor_copy(out=gw[:], in_=xw[:, s, :].bitcast(U32).indirect(picks(first, last)))
-                nc.vector.tensor_copy(out=gs[:], in_=x_plane[:, s, :].indirect(picks(first, last)))
+                nc.vector.tensor_copy(out=gw[:], in_=xw[:, s, :].bitcast(U32).indirect(picks))
+                nc.vector.tensor_copy(out=gs[:], in_=x_plane[:, s, :].indirect(picks))
                 for e in range(first, last):
                     words[e, s] = gw[:, (e - first) * C : (e - first + 1) * C]
                     scale_bytes[e, s] = gs[:, (e - first) * C : (e - first + 1) * C]
 
-        hidden, quantised = {}, {}
+        hidden, hidden_of, quantised = {}, {}, {}
         for first, last in QUANT_GROUPS:
-            tile = keep.tile([P, last - first, C * PACK], BF16, name="hidden%d" % first, align_bytes=64)
+            hidden[first] = keep.tile([P, last - first, C * PACK], BF16, name="hidden%d" % first, align_bytes=64)
             for e in range(first, last):
-                hidden[e] = tile
+                hidden_of[e] = hidden[first][:, e - first, :]
 
-        held = {}
+        def room_for_hidden(first, last, tag):
+            codes = keep.tile([P, (last - first) * C], U32, name="h_codes%d" % first, tag=tag, align_bytes=64)
+            plane = keep.tile([P, (last - first) * C], U8, name="h_plane%d" % first, align_bytes=64)
+            return first, codes, plane
 
-        def quantise_hidden(first, last):
-            base = min(first, E - 2)
-            if base not in held:
-                width = (last - first if base < E - 2 else 2) * C
-                tags = ("raw00" if base == E - 2 else "h_codes%d" % base, "h_plane%d" % base)
-                held[base] = (
-                    keep.tile([P, width], U32, name="h_codes%d" % base, tag=tags[0], align_bytes=64),
-                    keep.tile([P, width], U8, name="h_plane%d" % base, tag=tags[1], align_bytes=64),
-                )
-            codes, plane = held[base]
+        def quantise_hidden(room, first, last):
+            base, codes, plane = room
             span = slice((first - base) * C, (last - base) * C)
             nc.vector.quantize_mx(
                 out=codes[:, span].bitcast(FP8X4), scales=plane[:, span], in_=hidden[first][:].rearrange("p e c -> p (e c)")
@@ -154,7 +163,7 @@ def tile_moe_ogt_relu2_sigmoid_kernel(
         rects = {}
 
         def rectify(e):
-            pre = banks[e % 3]
+            pre = banks[e % DEPTH]
             for s in range(PASSES):
                 nc.tensor.matmul_mx(
                     out=pre[:],
@@ -165,11 +174,8 @@ def tile_moe_ogt_relu2_sigmoid_kernel(
                     start=(s == 0),
                     stop=(s == PASSES - 1),
                 )
-            if e == E - 1:
-                rect = keep.tile([P, PACK, P], F32, name="rect_last", tag="stage00", align_bytes=64)
-            else:
-                rect = ring.tile([P, PACK, P], F32, name="rect")
-            src = pre[:].rearrange("c (p t) -> c t p", t=PACK)
+            rect = ring.tile([P, PACK, P], F32, name="rect")
+            src = pre[:].rearrange("c (p d) -> c d p", d=PACK)
             if e == E - 1:
                 nc.vector.tensor_scalar_max(out=rect[:], in0=src, scalar1=0.0)
             else:
@@ -177,49 +183,66 @@ def tile_moe_ogt_relu2_sigmoid_kernel(
             rects[e] = rect
 
         def square(e):
-            rect = rects[e]
-            turned = banks[3 + e % 3]
-            for t in range(PACK):
-                nc.tensor.transpose(turned[:, t * C : (t + 1) * C], rect[:, t, :], ident[:])
-            first = [g[0] for g in QUANT_GROUPS if g[0] <= e][-1]
+            turned = banks[DEPTH + e % DEPTH]
+            for d in range(PACK):
+                nc.tensor.transpose(turned[:, d * C : (d + 1) * C], rects[e][:, d, :], ident[:])
             nc.scalar.activation(
-                out=hidden[e][:, e - first, :].rearrange("p (c t) -> p c t", t=PACK),
-                in_=turned[:].rearrange("p (t c) -> p c t", t=PACK),
+                out=hidden_of[e].rearrange("p (c d) -> p c d", d=PACK),
+                in_=turned[:].rearrange("p (d c) -> p c d", d=PACK),
                 func=ACT.Square,
             )
 
         woven = {}
 
-        def weave(s, h):
-            tile = keep.tile([P, HALF * PACK], BF16, name="woven%d%d" % (s, h), tag="stage%d%d" % (s, h), align_bytes=64)
-            woven[s, h] = tile[:]
+        def weave(s, half):
+            tile = keep.tile([P, HALF * PACK], BF16, name="woven%d%d" % (s, half), tag="stage%d%d" % (s, half), align_bytes=64)
+            woven[s, half] = tile[:]
             if s == 0:
-                nc.vector.tensor_copy(out=tile[:].rearrange("p (c j) -> p c j", j=PACK), in_=wg_raw[s, h].rearrange("p j c -> p c j"))
+                nc.vector.tensor_copy(
+                    out=tile[:].rearrange("p (n d) -> p n d", d=PACK), in_=wg_raw[s, half].rearrange("p d n -> p n d")
+                )
             else:
                 nc.scalar.copy(
-                    out=tile[:].rearrange("p (c i j) -> p c j i", i=4, j=PACK),
-                    in_=wg_raw[s, h].rearrange("p j (c i) -> p c j i", i=4),
+                    out=tile[:].rearrange("p (n m d) -> p n d m", m=4, d=PACK),
+                    in_=wg_raw[s, half].rearrange("p d (n m) -> p n d m", m=4),
                 )
 
+        wg_mx = [
+            (
+                keep.tile([P, N], U32, name="wg_codes%d" % s, align_bytes=64),
+                keep.tile([P, N], U8, name="wg_plane%d" % s, align_bytes=64),
+            )
+            for s in range(PASSES)
+        ]
+
+        def quantise_wg(s, half):
+            cols = slice(half * HALF, (half + 1) * HALF)
+            nc.vector.quantize_mx(out=wg_mx[s][0][:, cols].bitcast(FP8X4), scales=wg_mx[s][1][:, cols], in_=woven[s, half])
+
+        wide, pair, before_last, final = QUANT_GROUPS
         for step in range(E + AHEAD):
             if step < E:
                 rectify(step)
             if step >= AHEAD:
-                square(step - AHEAD)
-                if step - AHEAD == E - 1:
+                e = step - AHEAD
+                square(e)
+                if e == wide[1] - 1:
+                    quantise_hidden(room_for_hidden(*wide, "h_codes_wide"), *wide)
+                if e == pair[1] - 1:
                     weave(0, 0)
-                    quantise_hidden(E - 2, E - 1)
-                for first, last in QUANT_GROUPS:
-                    if last - 1 == step - AHEAD and first != E - 2:
-                        quantise_hidden(first, last)
+                    quantise_hidden(room_for_hidden(*pair, "raw00"), *pair)
+        quantise_wg(0, 0)
+        room = room_for_hidden(before_last[0], final[1], "stage00")
+        quantise_hidden(room, *before_last)
+        quantise_hidden(room, *final)
 
         ys = {}
 
-        def second_layer(j, first, last, bank, on_vector):
+        def second_layer(j, first, last, bank):
             for e in range(first, last):
                 nc.tensor.matmul_mx(
                     out=bank[:, (e - first) * C : (e - first + 1) * C],
-                    lhsT=w2[e // 4][:, e % 4, 2 * j * P : 2 * (j + 1) * P].bitcast(FP4X4),
+                    lhsT=w2[e // PER_BANK][:, e % PER_BANK, 2 * j * P : 2 * (j + 1) * P].bitcast(FP4X4),
                     lhsT_scale=w2_plane[:, e, j * P : (j + 1) * P],
                     rhs=quantised[e][0].bitcast(FP8X4),
                     rhs_scale=quantised[e][1],
@@ -229,39 +252,25 @@ def tile_moe_ogt_relu2_sigmoid_kernel(
             if j not in ys:
                 tag = "raw10" if j == BLOCKS - 1 else "y%d" % j
                 ys[j] = keep.tile([P, SLOTS], F32, name="y%d" % j, tag=tag, align_bytes=64)
-            dst, src = ys[j][:, first * C : last * C], bank[:, : (last - first) * C]
-            if on_vector:
-                nc.vector.tensor_copy(out=dst, in_=src)
-            else:
-                nc.scalar.copy(out=dst, in_=src)
+            nc.scalar.copy(out=ys[j][:, first * C : last * C], in_=bank[:, : (last - first) * C])
 
-        second_layer(0, 0, 4, banks[1], False)
-        second_layer(0, 4, 7, banks[3], False)
-        second_layer(0, 7, 8, banks[0], False)
-        second_layer(1, 0, 4, banks[3], False)
-        second_layer(1, 4, 8, banks[1], False)
-        second_layer(2, 0, 4, banks[0], False)
-        second_layer(2, 4, 8, banks[4], False)
+        second_layer(0, 0, PER_BANK, banks[1])
+        second_layer(0, PER_BANK, E - 1, banks[3])
+        second_layer(0, E - 1, E, banks[0])
+        second_layer(1, 0, PER_BANK, banks[3])
+        second_layer(1, PER_BANK, E, banks[1])
+        second_layer(2, 0, PER_BANK, banks[0])
+        second_layer(2, PER_BANK, E, banks[4])
 
-        opened = [keep.tile([P, T], F32, name="o%d" % j) for j in range(BLOCKS)]
-        matrix = {}
-
-        def quantise_gate_matrix(s):
-            codes = keep.tile([P, N], U32, name="wg_codes%d" % s, align_bytes=64)
-            plane = keep.tile([P, N], U8, name="wg_plane%d" % s, align_bytes=64)
-            for h in range(2):
-                cols = slice(h * HALF, (h + 1) * HALF)
-                nc.vector.quantize_mx(out=codes[:, cols].bitcast(FP8X4), scales=plane[:, cols], in_=woven[s, h])
-            matrix[s] = (codes, plane)
-
+        tanhs = [keep.tile([P, T], F32, name="tanh%d" % j) for j in range(BLOCKS)]
         gate_banks = [banks[b] for b in (5, 2, 0, 4)]
 
         def gate_pass(j, s):
             cols = slice(j * P, (j + 1) * P)
             nc.tensor.matmul_mx(
                 out=gate_banks[j][:],
-                lhsT=matrix[s][0][:, cols].bitcast(FP8X4),
-                lhsT_scale=matrix[s][1][:, cols],
+                lhsT=wg_mx[s][0][:, cols].bitcast(FP8X4),
+                lhsT_scale=wg_mx[s][1][:, cols],
                 rhs=xw[:, s, :].bitcast(FP8X4),
                 rhs_scale=x_plane[:, s, :],
                 start=(s == 0),
@@ -269,49 +278,54 @@ def tile_moe_ogt_relu2_sigmoid_kernel(
             )
 
         def fetch(j, r, part, first=0, last=T):
-            window = ys[j][:].indirect(back[r][:, first // 16 : last // 16])
+            window = ys[j][:].indirect(back[r][:, first // STRIPE : last // STRIPE])
             nc.vector.tensor_tensor(part[:, first:last], window, gates[:, r, first:last], ALU.mult)
 
         def add_turned(parts, bank, first=0, last=T):
             for c in range(first, last, P):
                 for r in range(2):
-                    nc.tensor.matmul(bank[:, c : c + P], parts[:, r, c : c + P], ident[:], start=(r == 0), stop=(r == 1), is_transpose=True)
+                    nc.tensor.matmul(
+                        bank[:, c : c + P], parts[:, r, c : c + P], ident[:], start=(r == 0), stop=(r == 1), is_transpose=True
+                    )
 
-        def turn_back(staged, bank, first=0, last=T):
-            nc.scalar.copy(out=staged[:, first:last], in_=bank[:, first:last])
+        def turn_back(stage, bank, first=0, last=T):
+            nc.scalar.activation(out=stage[:, first:last], in_=bank[:, first:last], func=ACT.Copy, scale=0.5)
             for c in range(first, last, P):
-                nc.tensor.transpose(bank[:, c : c + P], staged[:, c : c + P], ident[:])
+                nc.tensor.transpose(bank[:, c : c + P], stage[:, c : c + P], ident[:])
 
         def finish(j, bank, first=0, last=T):
             res = keep.tile([P, last - first], F32, name="res%d%d" % (j, first))
-            nc.vector.tensor_tensor(res[:], bank[:, first:last], opened[j][:, first:last], ALU.mult)
+            nc.vector.scalar_tensor_tensor(
+                out=res[:], in0=tanhs[j][:, first:last], scalar=1.0, in1=bank[:, first:last], op0=ALU.add, op1=ALU.mult
+            )
             nc.sync.dma_start(out=out[j * P : (j + 1) * P, first:last], in_=res[:])
 
         sums = [banks[b] for b in (6, 7, 3)]
         weave(0, 1)
-        quantise_gate_matrix(0)
+        quantise_wg(0, 1)
         early = keep.tile([P, 4, T], F32, name="early", tag="stage01", align_bytes=64)
         fetch(0, 0, early[:, 0, :])
         fetch(0, 1, early[:, 1, :])
         weave(1, 0)
         weave(1, 1)
-        second_layer(3, 0, 4, banks[3], False)
-        second_layer(3, 4, 8, banks[1], False)
+        second_layer(3, 0, PER_BANK, banks[3])
+        second_layer(3, PER_BANK, E, banks[1])
         for j in range(BLOCKS):
             gate_pass(j, 0)
         add_turned(early[:, 0:2, :], sums[0])
         fetch(1, 0, early[:, 2, :])
         fetch(1, 1, early[:, 3, :])
         add_turned(early[:, 2:4, :], sums[1])
-        quantise_gate_matrix(1)
+        quantise_wg(1, 0)
+        quantise_wg(1, 1)
         late = keep.tile([P, 4, T], F32, name="late", tag="stage11", align_bytes=64)
-        staged = keep.tile([P, 4, T], F32, name="staged", tag="stage10", align_bytes=64)
+        staged = keep.tile([P, BLOCKS, T], F32, name="staged", tag="stage10", align_bytes=64)
         fetch(2, 0, late[:, 0, :])
         fetch(2, 1, late[:, 1, :])
         turn_back(staged[:, 0, :], sums[0])
         for j in range(BLOCKS):
             gate_pass(j, 1)
-            nc.scalar.activation(out=opened[j][:], in_=gate_banks[j][:], func=ACT.Sigmoid)
+            nc.scalar.activation(out=tanhs[j][:], in_=gate_banks[j][:], func=ACT.Tanh, scale=0.5)
         turn_back(staged[:, 1, :], sums[1])
         add_turned(late[:, 0:2, :], sums[2])
         turn_back(staged[:, 2, :], sums[2])
@@ -321,7 +335,7 @@ def tile_moe_ogt_relu2_sigmoid_kernel(
             fetch(3, 1, late[:, 3, :], first, last)
             add_turned(late[:, 2:4, :], bank, first, last)
             turn_back(staged[:, 3, :], bank, first, last)
-        for j in range(BLOCKS - 1):
-            finish(j, sums[j])
+        for j, bank in enumerate(sums):
+            finish(j, bank)
         for first, last, bank in halves:
-            finish(3, bank, first, last)
+            finish(BLOCKS - 1, bank, first, last)

@@ -124,7 +124,7 @@ def tile_moe_ogt_relu2_sigmoid_kernel(
             for c in range(CHUNKS):
                 column = gate_cols[:, r * CHUNKS + c : r * CHUNKS + c + 1]
                 nc.tensor.transpose(banks[6 + r][:, c * P : (c + 1) * P], column.to_broadcast([P, P]), ident[:])
-            nc.scalar.copy(out=gates[:, r, :], in_=banks[6 + r][:])
+            nc.scalar.activation(out=gates[:, r, :], in_=banks[6 + r][:], func=ACT.Copy, scale=0.5)
 
         words, scale_bytes = {}, {}
         for first, last in GATHER_GROUPS:
@@ -289,16 +289,20 @@ def tile_moe_ogt_relu2_sigmoid_kernel(
                     )
 
         def turn_back(stage, bank, first=0, last=T):
-            nc.scalar.activation(out=stage[:, first:last], in_=bank[:, first:last], func=ACT.Copy, scale=0.5)
+            nc.scalar.copy(out=stage[:, first:last], in_=bank[:, first:last])
             for c in range(first, last, P):
                 nc.tensor.transpose(bank[:, c : c + P], stage[:, c : c + P], ident[:])
 
-        def finish(j, bank, first=0, last=T):
-            res = keep.tile([P, last - first], F32, name="res%d%d" % (j, first))
+        def finish(j, total, res, first=0, last=T):
             nc.vector.scalar_tensor_tensor(
-                out=res[:], in0=tanhs[j][:, first:last], scalar=1.0, in1=bank[:, first:last], op0=ALU.add, op1=ALU.mult
+                out=res[:, first:last],
+                in0=tanhs[j][:, first:last],
+                scalar=1.0,
+                in1=total[:, first:last],
+                op0=ALU.add,
+                op1=ALU.mult,
             )
-            nc.sync.dma_start(out=out[j * P : (j + 1) * P, first:last], in_=res[:])
+            nc.sync.dma_start(out=out[j * P : (j + 1) * P, first:last], in_=res[:, first:last])
 
         sums = [banks[b] for b in (6, 7, 3)]
         weave(0, 1)
@@ -319,7 +323,7 @@ def tile_moe_ogt_relu2_sigmoid_kernel(
         quantise_wg(1, 0)
         quantise_wg(1, 1)
         late = keep.tile([P, 4, T], F32, name="late", tag="stage11", align_bytes=64)
-        staged = keep.tile([P, BLOCKS, T], F32, name="staged", tag="stage10", align_bytes=64)
+        staged = keep.tile([P, BLOCKS - 1, T], F32, name="staged", tag="stage10", align_bytes=64)
         fetch(2, 0, late[:, 0, :])
         fetch(2, 1, late[:, 1, :])
         turn_back(staged[:, 0, :], sums[0])
@@ -329,13 +333,12 @@ def tile_moe_ogt_relu2_sigmoid_kernel(
         turn_back(staged[:, 1, :], sums[1])
         add_turned(late[:, 0:2, :], sums[2])
         turn_back(staged[:, 2, :], sums[2])
-        halves = ((0, T // 2, banks[1]), (T // 2, T, banks[5]))
         fetch(3, 0, late[:, 2, :])
-        for first, last, bank in halves:
-            fetch(3, 1, late[:, 3, :], first, last)
-            add_turned(late[:, 2:4, :], bank, first, last)
-            turn_back(staged[:, 3, :], bank, first, last)
+        fetch(3, 1, late[:, 3, :])
+        last_sum = keep.tile([P, T], F32, name="last_sum")
+        nc.gpsimd.tensor_tensor(last_sum[:], late[:, 2, :], late[:, 3, :], ALU.add)
         for j, bank in enumerate(sums):
-            finish(j, bank)
-        for first, last, bank in halves:
-            finish(BLOCKS - 1, bank, first, last)
+            finish(j, bank, keep.tile([P, T], F32, name="res%d" % j))
+        last_res = keep.tile([P, T], F32, name="last_res", tag="stage10", align_bytes=64)
+        for first in (0, T // 2):
+            finish(BLOCKS - 1, last_sum, last_res, first, first + T // 2)

@@ -106,14 +106,18 @@ def tile_moe_ogt_relu2_sigmoid_kernel(
                 wg_raw[s, half] = tile[:, :, half * HALF - first : (half + 1) * HALF - first]
 
         load_scale_rows(nc, w2_plane, w2_scales.rearrange("e s (q r) n -> r q (e s) n", r=4))
-        w2 = [keep.tile([P, PER_BANK, 2 * N], U8, name="w2_%d" % q, align_bytes=64) for q in range(E // PER_BANK)]
+        w2 = [keep.tile([P, E, 2 * HALF], U8, name="w2_%d" % half, align_bytes=64) for half in range(2)]
+
+        def load_w2(half):
+            src = w2_words[:, :, :, 2 * HALF * half : 2 * HALF * (half + 1)].rearrange("e s p b -> p (e s) b")
+            nc.sync.dma_start(out=w2[half][:].bitcast(I32), in_=src.bitcast(I32))
+
         load_wg(0, 0, HALF)
-        for q, tile in enumerate(w2):
-            src = w2_words[PER_BANK * q : PER_BANK * (q + 1)].rearrange("e s p b -> p (e s) b")
-            nc.sync.dma_start(out=tile[:].bitcast(I32), in_=src.bitcast(I32))
-        load_wg(0, HALF, N)
+        load_w2(0)
         nc.sync.dma_start(back[0][:], pos1)
         nc.sync.dma_start(back[1][:], pos2)
+        load_wg(0, HALF, N)
+        load_w2(1)
         load_wg(1, 0, N)
 
         gate_cols = keep.tile([P, 2 * CHUNKS], F32, name="gate_cols")
@@ -242,7 +246,7 @@ def tile_moe_ogt_relu2_sigmoid_kernel(
             for e in range(first, last):
                 nc.tensor.matmul_mx(
                     out=bank[:, (e - first) * C : (e - first + 1) * C],
-                    lhsT=w2[e // PER_BANK][:, e % PER_BANK, 2 * j * P : 2 * (j + 1) * P].bitcast(FP4X4),
+                    lhsT=w2[j // 2][:, e, 2 * (j % 2) * P : 2 * (j % 2 + 1) * P].bitcast(FP4X4),
                     lhsT_scale=w2_plane[:, e, j * P : (j + 1) * P],
                     rhs=quantised[e][0].bitcast(FP8X4),
                     rhs_scale=quantised[e][1],

@@ -96,29 +96,30 @@ def tile_moe_ogt_relu2_sigmoid_kernel(
 
         wg_raw = {}
 
-        def load_wg(s, first, last):
-            tile = keep.tile(
-                [P, PACK, last - first], F32, name="wg_raw%d%d" % (s, first), tag="raw%d%d" % (s, first // HALF), align_bytes=64
-            )
-            src = wg[s * K_PASS : (s + 1) * K_PASS, first:last].rearrange("(p d) n -> p d n", d=PACK)
+        def load_wg(s, half):
+            tile = keep.tile([P, PACK, HALF], F32, name="wg_raw%d%d" % (s, half), tag="raw%d%d" % (s, half), align_bytes=64)
+            src = wg[s * K_PASS : (s + 1) * K_PASS, half * HALF : (half + 1) * HALF].rearrange("(p d) n -> p d n", d=PACK)
             nc.sync.dma_start(out=tile[:], in_=src)
-            for half in range(first // HALF, last // HALF):
-                wg_raw[s, half] = tile[:, :, half * HALF - first : (half + 1) * HALF - first]
+            wg_raw[s, half] = tile[:]
 
         load_scale_rows(nc, w2_plane, w2_scales.rearrange("e s (q r) n -> r q (e s) n", r=4))
-        w2 = [keep.tile([P, E, 2 * HALF], U8, name="w2_%d" % half, align_bytes=64) for half in range(2)]
+        w2 = {}
 
-        def load_w2(half):
-            src = w2_words[:, :, :, 2 * HALF * half : 2 * HALF * (half + 1)].rearrange("e s p b -> p (e s) b")
-            nc.sync.dma_start(out=w2[half][:].bitcast(I32), in_=src.bitcast(I32))
+        def load_w2(first, last):
+            tile = keep.tile([P, E, 2 * P * (last - first)], U8, name="w2_%d" % first, align_bytes=64)
+            src = w2_words[:, :, :, 2 * P * first : 2 * P * last].rearrange("e s p b -> p (e s) b")
+            nc.sync.dma_start(out=tile[:].bitcast(I32), in_=src.bitcast(I32))
+            for j in range(first, last):
+                w2[j] = tile[:, :, 2 * P * (j - first) : 2 * P * (j - first + 1)]
 
-        load_wg(0, 0, HALF)
-        load_w2(0)
+        load_wg(0, 0)
+        load_w2(0, 1)
         nc.sync.dma_start(back[0][:], pos1)
         nc.sync.dma_start(back[1][:], pos2)
-        load_wg(0, HALF, N)
-        load_w2(1)
-        load_wg(1, 0, N)
+        load_wg(0, 1)
+        load_w2(1, BLOCKS)
+        load_wg(1, 0)
+        load_wg(1, 1)
 
         gate_cols = keep.tile([P, 2 * CHUNKS], F32, name="gate_cols")
         nc.tensor.transpose(banks[5][:, 0:P], gate_rows[:], ident[:])
@@ -246,7 +247,7 @@ def tile_moe_ogt_relu2_sigmoid_kernel(
             for e in range(first, last):
                 nc.tensor.matmul_mx(
                     out=bank[:, (e - first) * C : (e - first + 1) * C],
-                    lhsT=w2[j // 2][:, e, 2 * (j % 2) * P : 2 * (j % 2 + 1) * P].bitcast(FP4X4),
+                    lhsT=w2[j][:, e, :].bitcast(FP4X4),
                     lhsT_scale=w2_plane[:, e, j * P : (j + 1) * P],
                     rhs=quantised[e][0].bitcast(FP8X4),
                     rhs_scale=quantised[e][1],
@@ -254,7 +255,7 @@ def tile_moe_ogt_relu2_sigmoid_kernel(
                     stop=True,
                 )
             if j not in ys:
-                tag = "raw10" if j == BLOCKS - 1 else "y%d" % j
+                tag = "raw11" if j == BLOCKS - 1 else "y%d" % j
                 ys[j] = keep.tile([P, SLOTS], F32, name="y%d" % j, tag=tag, align_bytes=64)
             nc.scalar.copy(out=ys[j][:, first * C : last * C], in_=bank[:, : (last - first) * C])
 
@@ -281,20 +282,19 @@ def tile_moe_ogt_relu2_sigmoid_kernel(
                 stop=(s == PASSES - 1),
             )
 
-        def fetch(j, r, part, first=0, last=T):
-            window = ys[j][:].indirect(back[r][:, first // STRIPE : last // STRIPE])
-            nc.vector.tensor_tensor(part[:, first:last], window, gates[:, r, first:last], ALU.mult)
+        def fetch(j, r, part):
+            nc.vector.tensor_tensor(part, ys[j][:].indirect(back[r][:]), gates[:, r, :], ALU.mult)
 
-        def add_turned(parts, bank, first=0, last=T):
-            for c in range(first, last, P):
+        def add_turned(parts, bank):
+            for c in range(0, T, P):
                 for r in range(2):
                     nc.tensor.matmul(
                         bank[:, c : c + P], parts[:, r, c : c + P], ident[:], start=(r == 0), stop=(r == 1), is_transpose=True
                     )
 
-        def turn_back(stage, bank, first=0, last=T):
-            nc.scalar.copy(out=stage[:, first:last], in_=bank[:, first:last])
-            for c in range(first, last, P):
+        def turn_back(stage, bank):
+            nc.scalar.copy(out=stage, in_=bank[:])
+            for c in range(0, T, P):
                 nc.tensor.transpose(bank[:, c : c + P], stage[:, c : c + P], ident[:])
 
         def finish(j, total, res, first=0, last=T):

@@ -181,7 +181,7 @@ def tile_moe_ogt_relu2_sigmoid_kernel(
                 )
             rect = ring.tile([P, PACK, P], F32, name="rect")
             src = pre[:].rearrange("c (p d) -> c d p", d=PACK)
-            if e == E - 1:
+            if e >= E - 2:
                 nc.vector.tensor_scalar_max(out=rect[:], in0=src, scalar1=0.0)
             else:
                 nc.scalar.activation(out=rect[:], in_=src, func=ACT.Relu)

@@ -114,9 +114,9 @@ def tile_moe_ogt_relu2_sigmoid_kernel(
 
         load_wg(0, 0)
         load_w2(0, 1)
+        load_wg(0, 1)
         nc.sync.dma_start(back[0][:], pos1)
         nc.sync.dma_start(back[1][:], pos2)
-        load_wg(0, 1)
         load_w2(1, BLOCKS)
         load_wg(1, 0)
         load_wg(1, 1)
@@ -169,6 +169,27 @@ def tile_moe_ogt_relu2_sigmoid_kernel(
 
         def rectify(e):
             pre = banks[e % DEPTH]
+            if e == E - 2:
+                rect = ring.tile([P, PACK, P], F32, name="rect")
+                for half, bank in enumerate((banks[7], pre)):
+                    for s in range(PASSES):
+                        nc.tensor.matmul_mx(
+                            out=bank[:, :HALF],
+                            lhsT=words[e, s].bitcast(FP8X4),
+                            lhsT_scale=scale_bytes[e, s],
+                            rhs=w1[e, s][:, half * H : (half + 1) * H].bitcast(FP4X4),
+                            rhs_scale=w1_scale[e, s][:, half * HALF : (half + 1) * HALF],
+                            start=(s == 0),
+                            stop=(s == PASSES - 1),
+                        )
+                    src = bank[:, :HALF].rearrange("c (p d) -> c d p", d=PACK)
+                    dst = rect[:, :, half * P // 2 : (half + 1) * P // 2]
+                    if half == 0:
+                        nc.scalar.activation(out=dst, in_=src, func=ACT.Relu)
+                    else:
+                        nc.vector.tensor_scalar_max(out=dst, in0=src, scalar1=0.0)
+                rects[e] = rect
+                return
             for s in range(PASSES):
                 nc.tensor.matmul_mx(
                     out=pre[:],
@@ -263,7 +284,7 @@ def tile_moe_ogt_relu2_sigmoid_kernel(
         second_layer(0, PER_BANK, E - 1, banks[3])
         second_layer(0, E - 1, E, banks[0])
         second_layer(1, 0, PER_BANK, banks[3])
-        second_layer(1, PER_BANK, E, banks[1])
+        second_layer(1, PER_BANK, E, banks[6])
         second_layer(2, 0, PER_BANK, banks[0])
         second_layer(2, PER_BANK, E, banks[4])
 

@@ -169,7 +169,7 @@ def tile_moe_ogt_relu2_sigmoid_kernel(
 
         def rectify(e):
             pre = banks[e % DEPTH]
-            if e == E - 2:
+            if e == E - 1:
                 rect = ring.tile([P, PACK, P], F32, name="rect")
                 for half, bank in enumerate((banks[7], pre)):
                     for s in range(PASSES):

from contextlib import ExitStack

import concourse.mybir as mybir
from concourse.masks import make_identity

K, T, E, C, H, N = 1024, 512, 8, 128, 512, 512
FLOPS = 2 * K * N * T + 2 * E * C * (K * H + H * N)

F32 = mybir.dt.float32
BF16 = mybir.dt.bfloat16
I32 = mybir.dt.int32
U32 = mybir.dt.uint32
U16 = mybir.dt.uint16
U8 = mybir.dt.uint8
FP8X4 = mybir.dt.float8_e4m3fn_x4
FP4X4 = mybir.dt.float4_e2m1fn_x4
ACT = mybir.ActivationFunctionType
ALU = mybir.AluOpType

P = 128
PACK = 4
K_PASS = P * PACK
PASSES = K // K_PASS
SLOTS = E * C
BLOCKS = N // P
CHUNKS = T // P
HALF = N // 2
BANK = 512
PER_BANK = BANK // C
STRIPE = 16
GATHER_GROUPS = ((0, 2), (2, 4), (4, 6), (6, 7), (7, 8))
W1_GROUPS = ((0, 2), (2, 4), (4, 6), (6, 8))
W1_SCALE_GROUPS = ((0, 4), (4, 8))
QUANT_GROUPS = ((0, 4), (4, 6), (6, 7), (7, 8))
AHEAD = 2
DEPTH = AHEAD + 1


def load_scale_rows(nc, plane, rows):
    for r in range(4):
        nc.sync.dma_start(out=plane[r:P:32, :, :].bitcast(I32), in_=rows[r].bitcast(I32))


def tile_moe_ogt_relu2_sigmoid_kernel(
    tc, x_words, x_scales, wg, w1_words, w1_scales, w2_words, w2_scales, gate, offs, pos1, pos2, out
):
    nc = tc.nc
    with ExitStack() as ctx:
        keep = ctx.enter_context(tc.tile_pool(name="keep", bufs=1))
        ring = ctx.enter_context(tc.tile_pool(name="ring", bufs=DEPTH))
        psum = ctx.enter_context(tc.psum_pool(name="psum", bufs=1))
        banks = [psum.tile([P, BANK], F32, name="bank%d" % b) for b in range(8)]

        x_plane = keep.tile([P, PASSES, T], U8, name="x_plane", align_bytes=64)
        w1_planes = [
            keep.tile([P, (last - first) * PASSES, H], U8, name="w1_plane%d" % first, align_bytes=64)
            for first, last in W1_SCALE_GROUPS
        ]
        w2_plane = keep.tile([P, E, N], U8, name="w2_plane", align_bytes=64)
        gate_rows = keep.tile([P, P], F32, name="gate_rows")
        nc.gpsimd.memset(gate_rows[:], 0.0)
        nc.gpsimd.memset(x_plane[:].rearrange("p s t -> p (s t)").bitcast(I32), 0)
        for plane in w1_planes:
            nc.vector.memset(plane[:].rearrange("p s t -> p (s t)").bitcast(I32), 0)

        ident = keep.tile([P, P], F32, name="ident")
        make_identity(nc, ident[:])
        nc.gpsimd.memset(w2_plane[:].rearrange("p s t -> p (s t)").bitcast(I32), 0)

        slot_list = keep.tile([P, SLOTS // STRIPE], U16, name="slot_list")
        back = [keep.tile([P, T // STRIPE], U16, name="back%d" % r) for r in range(2)]
        xw = keep.tile([P, PASSES, T], I32, name="xw", align_bytes=64)
        nc.sync.dma_start(out=xw[:], in_=x_words.rearrange("s p t d -> p s (t d)").bitcast(I32))
        gate_runs = gate.rearrange("r p (c t) -> (r p c) t", t=P)
        nc.sync.dma_start(out=gate_rows[0 : 2 * CHUNKS, :], in_=gate_runs[0 : 2 * P * CHUNKS : P + 1, :])
        load_scale_rows(nc, x_plane, x_scales.rearrange("s (q r) t -> r q s t", r=4))
        nc.sync.dma_start(slot_list[:], offs)

        w1, w1_scale = {}, {}

        def load_w1(first, last):
            tile = keep.tile([P, (last - first) * PASSES, 2 * H], U8, name="w1_%d" % first, align_bytes=64)
            src = w1_words[first:last].rearrange("e s p b -> p (e s) b")
            nc.sync.dma_start(out=tile[:].bitcast(I32), in_=src.bitcast(I32))
            for e in range(first, last):
                for s in range(PASSES):
                    w1[e, s] = tile[:, (e - first) * PASSES + s, :]

        for run, (first, last) in enumerate(W1_SCALE_GROUPS):
            load_w1(*W1_GROUPS[2 * run])
            load_scale_rows(nc, w1_planes[run], w1_scales[first:last].rearrange("e s (q r) i -> r q (e s) i", r=4))
            load_w1(*W1_GROUPS[2 * run + 1])
            for e in range(first, last):
                for s in range(PASSES):
                    w1_scale[e, s] = w1_planes[run][:, (e - first) * PASSES + s, :]

        wg_raw = {}

        def load_wg(s, half):
            tile = keep.tile([P, PACK, HALF], F32, name="wg_raw%d%d" % (s, half), tag="raw%d%d" % (s, half), align_bytes=64)
            src = wg[s * K_PASS : (s + 1) * K_PASS, half * HALF : (half + 1) * HALF].rearrange("(p d) n -> p d n", d=PACK)
            nc.sync.dma_start(out=tile[:], in_=src)
            wg_raw[s, half] = tile[:]

        load_scale_rows(nc, w2_plane, w2_scales.rearrange("e s (q r) n -> r q (e s) n", r=4))
        w2 = {}

        def load_w2(first, last):
            tile = keep.tile([P, E, 2 * P * (last - first)], U8, name="w2_%d" % first, align_bytes=64)
            src = w2_words[:, :, :, 2 * P * first : 2 * P * last].rearrange("e s p b -> p (e s) b")
            nc.sync.dma_start(out=tile[:].bitcast(I32), in_=src.bitcast(I32))
            for j in range(first, last):
                w2[j] = tile[:, :, 2 * P * (j - first) : 2 * P * (j - first + 1)]

        load_wg(0, 0)
        load_w2(0, 1)
        load_wg(0, 1)
        nc.sync.dma_start(back[0][:], pos1)
        nc.sync.dma_start(back[1][:], pos2)
        load_w2(1, BLOCKS)
        load_wg(1, 0)
        load_wg(1, 1)

        gate_cols = keep.tile([P, 2 * CHUNKS], F32, name="gate_cols")
        nc.tensor.transpose(banks[5][:, 0:P], gate_rows[:], ident[:])
        nc.scalar.copy(out=gate_cols[:], in_=banks[5][:, 0 : 2 * CHUNKS])
        gates = keep.tile([P, 2, T], F32, name="gates")
        for r in range(2):
            for c in range(CHUNKS):
                column = gate_cols[:, r * CHUNKS + c : r * CHUNKS + c + 1]
                nc.tensor.transpose(banks[6 + r][:, c * P : (c + 1) * P], column.to_broadcast([P, P]), ident[:])
            nc.scalar.activation(out=gates[:, r, :], in_=banks[6 + r][:], func=ACT.Copy, scale=0.5)

        words, scale_bytes = {}, {}
        for first, last in GATHER_GROUPS:
            width = (last - first) * C
            picks = slot_list[:, first * C // STRIPE : last * C // STRIPE]
            for s in range(PASSES):
                gw = keep.tile([P, width], U32, name="gw%d%d" % (first, s), align_bytes=64)
                gs = keep.tile([P, width], U8, name="gs%d%d" % (first, s), align_bytes=64)
                nc.vector.tensor_copy(out=gw[:], in_=xw[:, s, :].bitcast(U32).indirect(picks))
                nc.vector.tensor_copy(out=gs[:], in_=x_plane[:, s, :].indirect(picks))
                for e in range(first, last):
                    words[e, s] = gw[:, (e - first) * C : (e - first + 1) * C]
                    scale_bytes[e, s] = gs[:, (e - first) * C : (e - first + 1) * C]

        hidden, hidden_of, quantised = {}, {}, {}
        for first, last in QUANT_GROUPS:
            hidden[first] = keep.tile([P, last - first, C * PACK], BF16, name="hidden%d" % first, align_bytes=64)
            for e in range(first, last):
                hidden_of[e] = hidden[first][:, e - first, :]

        def room_for_hidden(first, last, tag):
            codes = keep.tile([P, (last - first) * C], U32, name="h_codes%d" % first, tag=tag, align_bytes=64)
            plane = keep.tile([P, (last - first) * C], U8, name="h_plane%d" % first, align_bytes=64)
            return first, codes, plane

        def quantise_hidden(room, first, last):
            base, codes, plane = room
            span = slice((first - base) * C, (last - base) * C)
            nc.vector.quantize_mx(
                out=codes[:, span].bitcast(FP8X4), scales=plane[:, span], in_=hidden[first][:].rearrange("p e c -> p (e c)")
            )
            for e in range(first, last):
                cols = slice((e - base) * C, (e - base + 1) * C)
                quantised[e] = (codes[:, cols], plane[:, cols])

        rects = {}

        def rectify(e):
            pre = banks[e % DEPTH]
            if e == E - 1:
                rect = ring.tile([P, PACK, P], F32, name="rect")
                for half, bank in enumerate((banks[7], pre)):
                    for s in range(PASSES):
                        nc.tensor.matmul_mx(
                            out=bank[:, :HALF],
                            lhsT=words[e, s].bitcast(FP8X4),
                            lhsT_scale=scale_bytes[e, s],
                            rhs=w1[e, s][:, half * H : (half + 1) * H].bitcast(FP4X4),
                            rhs_scale=w1_scale[e, s][:, half * HALF : (half + 1) * HALF],
                            start=(s == 0),
                            stop=(s == PASSES - 1),
                        )
                    src = bank[:, :HALF].rearrange("c (p d) -> c d p", d=PACK)
                    dst = rect[:, :, half * P // 2 : (half + 1) * P // 2]
                    if half == 0:
                        nc.scalar.activation(out=dst, in_=src, func=ACT.Relu)
                    else:
                        nc.vector.tensor_scalar_max(out=dst, in0=src, scalar1=0.0)
                rects[e] = rect
                return
            for s in range(PASSES):
                nc.tensor.matmul_mx(
                    out=pre[:],
                    lhsT=words[e, s].bitcast(FP8X4),
                    lhsT_scale=scale_bytes[e, s],
                    rhs=w1[e, s].bitcast(FP4X4),
                    rhs_scale=w1_scale[e, s],
                    start=(s == 0),
                    stop=(s == PASSES - 1),
                )
            rect = ring.tile([P, PACK, P], F32, name="rect")
            src = pre[:].rearrange("c (p d) -> c d p", d=PACK)
            if e >= E - 2:
                nc.vector.tensor_scalar_max(out=rect[:], in0=src, scalar1=0.0)
            else:
                nc.scalar.activation(out=rect[:], in_=src, func=ACT.Relu)
            rects[e] = rect

        def square(e):
            turned = banks[DEPTH + e % DEPTH]
            for d in range(PACK):
                nc.tensor.transpose(turned[:, d * C : (d + 1) * C], rects[e][:, d, :], ident[:])
            nc.scalar.activation(
                out=hidden_of[e].rearrange("p (c d) -> p c d", d=PACK),
                in_=turned[:].rearrange("p (d c) -> p c d", d=PACK),
                func=ACT.Square,
            )

        woven = {}

        def weave(s, half):
            tile = keep.tile([P, HALF * PACK], BF16, name="woven%d%d" % (s, half), tag="stage%d%d" % (s, half), align_bytes=64)
            woven[s, half] = tile[:]
            if s == 0:
                nc.vector.tensor_copy(
                    out=tile[:].rearrange("p (n d) -> p n d", d=PACK), in_=wg_raw[s, half].rearrange("p d n -> p n d")
                )
            else:
                nc.scalar.copy(
                    out=tile[:].rearrange("p (n m d) -> p n d m", m=4, d=PACK),
                    in_=wg_raw[s, half].rearrange("p d (n m) -> p n d m", m=4),
                )

        wg_mx = [
            (
                keep.tile([P, N], U32, name="wg_codes%d" % s, align_bytes=64),
                keep.tile([P, N], U8, name="wg_plane%d" % s, align_bytes=64),
            )
            for s in range(PASSES)
        ]

        def quantise_wg(s, half):
            cols = slice(half * HALF, (half + 1) * HALF)
            nc.vector.quantize_mx(out=wg_mx[s][0][:, cols].bitcast(FP8X4), scales=wg_mx[s][1][:, cols], in_=woven[s, half])

        wide, pair, before_last, final = QUANT_GROUPS
        for step in range(E + AHEAD):
            if step < E:
                rectify(step)
            if step >= AHEAD:
                e = step - AHEAD
                square(e)
                if e == wide[1] - 1:
                    quantise_hidden(room_for_hidden(*wide, "h_codes_wide"), *wide)
                if e == pair[1] - 1:
                    weave(0, 0)
                    quantise_hidden(room_for_hidden(*pair, "raw00"), *pair)
        quantise_wg(0, 0)
        room = room_for_hidden(before_last[0], final[1], "stage00")
        quantise_hidden(room, *before_last)
        quantise_hidden(room, *final)

        ys = {}

        def second_layer(j, first, last, bank):
            for e in range(first, last):
                nc.tensor.matmul_mx(
                    out=bank[:, (e - first) * C : (e - first + 1) * C],
                    lhsT=w2[j][:, e, :].bitcast(FP4X4),
                    lhsT_scale=w2_plane[:, e, j * P : (j + 1) * P],
                    rhs=quantised[e][0].bitcast(FP8X4),
                    rhs_scale=quantised[e][1],
                    start=True,
                    stop=True,
                )
            if j not in ys:
                tag = "raw11" if j == BLOCKS - 1 else "y%d" % j
                ys[j] = keep.tile([P, SLOTS], F32, name="y%d" % j, tag=tag, align_bytes=64)
            nc.scalar.copy(out=ys[j][:, first * C : last * C], in_=bank[:, : (last - first) * C])

        second_layer(0, 0, PER_BANK, banks[1])
        second_layer(0, PER_BANK, E - 1, banks[3])
        second_layer(0, E - 1, E, banks[0])
        second_layer(1, 0, PER_BANK, banks[3])
        second_layer(1, PER_BANK, E, banks[6])
        second_layer(2, 0, PER_BANK, banks[0])
        second_layer(2, PER_BANK, E, banks[4])

        tanhs = [keep.tile([P, T], F32, name="tanh%d" % j) for j in range(BLOCKS)]
        gate_banks = [banks[b] for b in (5, 2, 0, 4)]

        def gate_pass(j, s):
            cols = slice(j * P, (j + 1) * P)
            nc.tensor.matmul_mx(
                out=gate_banks[j][:],
                lhsT=wg_mx[s][0][:, cols].bitcast(FP8X4),
                lhsT_scale=wg_mx[s][1][:, cols],
                rhs=xw[:, s, :].bitcast(FP8X4),
                rhs_scale=x_plane[:, s, :],
                start=(s == 0),
                stop=(s == PASSES - 1),
            )

        def fetch(j, r, part):
            nc.vector.tensor_tensor(part, ys[j][:].indirect(back[r][:]), gates[:, r, :], ALU.mult)

        def add_turned(parts, bank):
            for c in range(0, T, P):
                for r in range(2):
                    nc.tensor.matmul(
                        bank[:, c : c + P], parts[:, r, c : c + P], ident[:], start=(r == 0), stop=(r == 1), is_transpose=True
                    )

        def turn_back(stage, bank):
            nc.scalar.copy(out=stage, in_=bank[:])
            for c in range(0, T, P):
                nc.tensor.transpose(bank[:, c : c + P], stage[:, c : c + P], ident[:])

        def finish(j, total, res, first=0, last=T):
            nc.vector.scalar_tensor_tensor(
                out=res[:, first:last],
                in0=tanhs[j][:, first:last],
                scalar=1.0,
                in1=total[:, first:last],
                op0=ALU.add,
                op1=ALU.mult,
            )
            nc.sync.dma_start(out=out[j * P : (j + 1) * P, first:last], in_=res[:, first:last])

        sums = [banks[b] for b in (6, 7, 3)]
        weave(0, 1)
        quantise_wg(0, 1)
        early = keep.tile([P, 4, T], F32, name="early", tag="stage01", align_bytes=64)
        fetch(0, 0, early[:, 0, :])
        fetch(0, 1, early[:, 1, :])
        weave(1, 0)
        weave(1, 1)
        second_layer(3, 0, PER_BANK, banks[3])
        second_layer(3, PER_BANK, E, banks[1])
        for j in range(BLOCKS):
            gate_pass(j, 0)
        add_turned(early[:, 0:2, :], sums[0])
        fetch(1, 0, early[:, 2, :])
        fetch(1, 1, early[:, 3, :])
        add_turned(early[:, 2:4, :], sums[1])
        quantise_wg(1, 0)
        quantise_wg(1, 1)
        late = keep.tile([P, 4, T], F32, name="late", tag="stage11", align_bytes=64)
        staged = keep.tile([P, BLOCKS - 1, T], F32, name="staged", tag="stage10", align_bytes=64)
        fetch(2, 0, late[:, 0, :])
        fetch(2, 1, late[:, 1, :])
        turn_back(staged[:, 0, :], sums[0])
        for j in range(BLOCKS):
            gate_pass(j, 1)
            nc.scalar.activation(out=tanhs[j][:], in_=gate_banks[j][:], func=ACT.Tanh, scale=0.5)
        turn_back(staged[:, 1, :], sums[1])
        add_turned(late[:, 0:2, :], sums[2])
        turn_back(staged[:, 2, :], sums[2])
        fetch(3, 0, late[:, 2, :])
        fetch(3, 1, late[:, 3, :])
        last_sum = keep.tile([P, T], F32, name="last_sum")
        nc.gpsimd.tensor_tensor(last_sum[:], late[:, 2, :], late[:, 3, :], ALU.add)
        for j, bank in enumerate(sums):
            finish(j, bank, keep.tile([P, T], F32, name="res%d" % j))
        last_res = keep.tile([P, T], F32, name="last_res", tag="stage10", align_bytes=64)
        for first in (0, T // 2):
            finish(BLOCKS - 1, last_sum, last_res, first, first + T // 2)
